import numpy as np
import ml_dtypes


def mxq(x, axis, fmt="e4m3"):
    dtype, down = {"e4m3": (ml_dtypes.float8_e4m3fn, 7), "e5m2": (ml_dtypes.float8_e5m2, 14)}[fmt]
    v = np.moveaxis(np.asarray(x, np.float32).astype(ml_dtypes.bfloat16).astype(np.float64), axis, -1)
    blocks = v.reshape(v.shape[:-1] + (-1, 32))
    amax = np.abs(blocks).max(-1, keepdims=True)
    byte = np.maximum(np.where(amax > 0, np.frexp(amax)[1] - 1 + 127, 0) - down, 1)
    scale = np.exp2(byte - 127.0)
    codes = (blocks / scale).astype(np.float32).astype(dtype).astype(np.float64)
    return np.moveaxis((codes * scale).reshape(v.shape), -1, axis)


WIDE = False


def mx_kscale(k):
    if not WIDE:
        return np.ones(k)
    levels = np.array([10, -10, 5, -5, 0])
    if k % 512:
        return np.exp2(np.random.permutation(np.resize(levels, k // 32))).repeat(32)
    a = np.empty((k // 512, 16))
    for p in range(k // 512):
        a[p, :8] = np.random.permutation(np.resize(levels, 8))
        for g in range(8):
            far = levels[np.abs(levels - a[p, g]) >= 10]
            a[p, g + 8] = far[np.random.randint(len(far))]
    return np.exp2(a.ravel()).repeat(32)


def f64(x):
    return np.asarray(x).astype(np.float64)


def striped(idx):
    return np.tile(idx.reshape(-1, 16).T, (8, 1)).astype(np.uint16)


def unstriped(offs):
    return offs[:16].T.reshape(-1).astype(np.int64)


def pack_weight(w):
    k, n = w.shape
    w = f64(np.asarray(w, np.float32).astype(ml_dtypes.bfloat16)).reshape(k // 32, 32, n)
    amax = np.abs(w).max(1)
    byte = np.clip(np.where(amax > 0, np.frexp(amax)[1] - 1 + 127 - 7, 1), 1, 254)
    scaled = (w * np.exp2(127.0 - byte)[:, None, :]).reshape(k, n).astype(np.float32)
    words = np.ascontiguousarray(scaled.reshape(k // 512, 128, 4, n).transpose(0, 1, 3, 2)).astype(ml_dtypes.float8_e4m3fn).view(np.uint8)
    return words, np.ascontiguousarray(byte.astype(np.uint8).reshape(k // 512, 16, n))


def unpack_weight(words, scales):
    g, p, n, _ = words.shape
    vals = np.ascontiguousarray(words).view(ml_dtypes.float8_e4m3fn).astype(np.float64) * np.repeat(np.exp2(scales.astype(np.float64) - 127.0), 8, axis=1)[..., None]
    return vals.transpose(0, 1, 3, 2).reshape(g * 512, n)


def gelu(v):
    return 0.5 * v * (1.0 + np.tanh(np.sqrt(2.0 / np.pi) * (v + 0.044715 * v**3)))


K, T, S, H, N = 1024, 1024, 512, 512, 256
P = 2 ** 7


def setup_inputs():
    n = np.random.standard_normal
    s = mx_kscale(K)[:, None]
    u = mx_kscale(H)
    packed_xT = pack_weight(n((K, T)) * s)
    packed_w2 = pack_weight(n((H, N)) / np.sqrt(H) / u[:, None])
    return {
        "x_words": packed_xT[0],
        "x_scales": packed_xT[1],
        "gate": np.tile(np.random.uniform(0.2, 1.0, S), (P, 1)).astype(np.float32),
        "res": n((N, T)).astype(np.float32),
        "w1": (n((K, H)) / np.sqrt(K) / s * u).astype(np.float32),
        "w2_words": packed_w2[0],
        "w2_scales": packed_w2[1],
        "offs": striped(np.random.permutation(T)[:S]),
    }


def reference(x_words, x_scales, gate, res, w1, w2_words, w2_scales, offs):
    r = f64(res)[:, unstriped(offs)]
    xq = unpack_weight(x_words, x_scales)[:, unstriped(offs)]
    h = gelu(mxq(f64(w1), 0, "e4m3").T @ xq)
    y = unpack_weight(w2_words, w2_scales).T @ mxq(h, 0, "e4m3")
    out = f64(res).copy()
    out[:, unstriped(offs)] = r + y * f64(gate)[:1]
    return out

@@ -1,0 +1,236 @@
+from contextlib import ExitStack
+
+import concourse.mybir as mybir
+from concourse.masks import make_identity
+
+K, T, S, H, N = 1024, 1024, 512, 512, 256
+FLOPS = 2 * S * H * (K + N)
+
+F32 = mybir.dt.float32
+BF16 = mybir.dt.bfloat16
+I32 = mybir.dt.int32
+U32 = mybir.dt.uint32
+U16 = mybir.dt.uint16
+U8 = mybir.dt.uint8
+FP8X4 = mybir.dt.float8_e4m3fn_x4
+GELU = mybir.ActivationFunctionType.Gelu_apprx_tanh
+COPY = mybir.ActivationFunctionType.Copy
+ADD = mybir.AluOpType.add
+MULT = mybir.AluOpType.mult
+
+P = 128
+PACK = 4
+K_PASS = P * PACK
+PASSES = K // K_PASS
+CHUNK = 128
+CHUNKS = S // CHUNK
+BLOCKS = N // P
+HALF = H // 2
+LIST_ROWS = 16
+
+
+def tile_picked_modres_mlpgelu_p_kernel(tc, x_words, x_scales, gate, res, w1, w2_words, w2_scales, offs, out):
+    nc = tc.nc
+    with ExitStack() as ctx:
+        keep = ctx.enter_context(tc.tile_pool(name="keep", bufs=1))
+        psum = ctx.enter_context(tc.psum_pool(name="psum", bufs=1))
+
+        offsets = keep.tile([P, S // LIST_ROWS], U16, name="offsets")
+
+        def entries(first, last):
+            return offsets[:, first // LIST_ROWS : last // LIST_ROWS]
+
+        xs_window = keep.tile([P, T], U8, name="xs_window", align_bytes=64)
+        warm_in = keep.tile([P, 8], F32, name="warm_in")
+        warm_out = keep.tile([P, 8], F32, name="warm_out")
+        identity = keep.tile([P, P], F32, name="identity")
+        nc.vector.memset(xs_window[:].bitcast(I32), 0)
+        nc.vector.memset(warm_in[:], 0.0)
+        nc.scalar.activation(warm_out[:], warm_in[:], GELU)
+        make_identity(nc, identity[:])
+
+        w1_raw = {}
+
+        def load_w1(z, half):
+            raw = keep.tile([P, PACK, HALF], F32, name="w1_raw_%d_%d" % (z, half), align_bytes=64)
+            rows = w1[z * K_PASS : (z + 1) * K_PASS, half * HALF : (half + 1) * HALF]
+            nc.sync.dma_start(out=raw[:], in_=rows.rearrange("(p j) c -> p j c", j=PACK))
+            w1_raw[z, half] = raw
+
+        nc.sync.dma_start(offsets[:], offs)
+        load_w1(0, 0)
+        for q in range(4):
+            nc.sync.dma_start(
+                out=xs_window[32 * q : 32 * q + 4 * PASSES, :].bitcast(I32),
+                in_=x_scales[:, 4 * q : 4 * q + 4, :].bitcast(I32),
+            )
+        load_w1(0, 1)
+        load_w1(1, 0)
+        x_window = []
+        for z in range(PASSES):
+            window = keep.tile([P, T], U32, name="x_window_%d" % z, align_bytes=64)
+            nc.sync.dma_start(
+                out=window[:].bitcast(I32),
+                in_=x_words[z].rearrange("p n t -> p (n t)").bitcast(I32),
+            )
+            x_window.append(window)
+        load_w1(1, 1)
+        stream = [keep.tile([P, T], F32, name="stream_%d" % b, align_bytes=64) for b in range(BLOCKS)]
+        for b in range(BLOCKS):
+            nc.sync.dma_start(out=stream[b][:], in_=res[b * P : (b + 1) * P, :])
+
+        x_plane = keep.tile([P, S], U8, name="x_plane", align_bytes=64)
+        nc.vector.tensor_copy(x_plane[:], xs_window[:].indirect(offsets[:]))
+
+        grouped = [keep.tile([P, PACK, P, PACK], BF16, name="w1_grouped_%d" % z, align_bytes=64) for z in range(PASSES)]
+        w1_codes = [keep.tile([P, H], U32, name="w1_codes_%d" % z, align_bytes=64) for z in range(PASSES)]
+        w1_plane = [keep.tile([P, H], U8, name="w1_plane_%d" % z, align_bytes=64) for z in range(PASSES)]
+
+        def round_w1(copy, z, half, t0, t1):
+            dst = grouped[z][:, t0:t1, half * 64 : (half + 1) * 64, :].rearrange("p t m j -> p m j t")
+            src = w1_raw[z, half][:].rearrange("p j (m t) -> p m j t", t=PACK)[:, :, :, t0:t1]
+            copy(out=dst, in_=src)
+
+        def quantize_w1(z, t0, t1):
+            nc.vector.quantize_mx(
+                out=w1_codes[z][:, t0 * P : t1 * P].bitcast(FP8X4),
+                scales=w1_plane[z][:, t0 * P : t1 * P],
+                in_=grouped[z][:, t0:t1, :, :].rearrange("p t m j -> p (t m j)"),
+            )
+
+        round_w1(nc.scalar.copy, 0, 0, 0, PACK)
+        round_w1(nc.scalar.copy, 0, 1, 0, PACK)
+        quantize_w1(0, 0, PACK)
+        round_w1(nc.scalar.copy, 1, 0, 0, PACK)
+
+        x_codes = [keep.tile([P, S], U32, name="x_codes_%d" % z, align_bytes=64) for z in range(PASSES)]
+        for z in range(PASSES):
+            nc.vector.tensor_copy(x_codes[z][:], x_window[z][:].indirect(offsets[:]))
+
+        round_w1(nc.vector.tensor_copy, 1, 1, 0, 2)
+        round_w1(nc.scalar.copy, 1, 1, 2, PACK)
+        quantize_w1(1, 0, 2)
+        quantize_w1(1, 2, PACK)
+
+        w2_plane = keep.tile([P, N], U8, name="w2_plane", tag="w1_raw_0_0", align_bytes=64)
+        nc.gpsimd.memset(w2_plane[:].bitcast(I32), 0)
+        for q in range(4):
+            nc.scalar.dma_start(
+                out=w2_plane[32 * q : 32 * q + 4, :].bitcast(I32),
+                in_=w2_scales[0, 4 * q : 4 * q + 4, :].bitcast(I32),
+            )
+        gate_rows = keep.tile([P, P], F32, name="gate_rows", tag="w1_raw_0_1", align_bytes=64)
+        nc.gpsimd.memset(gate_rows[:], 0.0)
+        nc.scalar.dma_start(out=gate_rows[0:CHUNKS, :], in_=gate[0].rearrange("(c p) -> c p", p=P))
+        gate_first = keep.tile([P, CHUNK], F32, name="gate_first", tag="w1_raw_1_0", align_bytes=64)
+        nc.scalar.dma_start(out=gate_first[:], in_=gate[:, 0:CHUNK])
+        w2_codes = keep.tile([P, N], U32, name="w2_codes", tag="x_window_0", align_bytes=64)
+        nc.scalar.dma_start(
+            out=w2_codes[:].bitcast(I32),
+            in_=w2_words[0].rearrange("p n t -> p (n t)").bitcast(I32),
+        )
+        gate_bank = psum.tile([P, P], F32, name="gate_bank", tag="turn_odd")
+        nc.tensor.transpose(gate_bank[:], gate_rows[:], identity[:])
+        gate_cols = keep.tile([P, CHUNKS], F32, name="gate_cols")
+        nc.scalar.copy(out=gate_cols[:], in_=gate_bank[:, 0:CHUNKS])
+
+        old_upper = keep.tile([P, S], F32, name="old_upper", align_bytes=64)
+        nc.vector.tensor_copy(old_upper[:], stream[0][:].indirect(offsets[:]))
+        old_lower_first = keep.tile([P, CHUNK], F32, name="old_lower_first", align_bytes=64)
+        nc.vector.tensor_copy(old_lower_first[:], stream[1][:].indirect(entries(0, CHUNK)))
+
+        turned_last = psum.tile([P, 2 * CHUNK], F32, name="turned_last")
+        h_tags = ["h_a", "h_b", "h_c", "h_b"]
+        y_tags = ["y_even", "y_odd", "y_even", "y_odd"]
+        turn_tags = ["h_a", "turn_odd", "h_a", "turn_odd"]
+        h_mx = {}
+
+        def hidden(c):
+            cols = slice(c * CHUNK, (c + 1) * CHUNK)
+            bank = psum.tile([P, PACK, CHUNK], F32, name="h_bank", tag=h_tags[c])
+            for t in range(PACK):
+                rows = slice(t * P, (t + 1) * P)
+                for z in range(PASSES):
+                    nc.tensor.matmul_mx(
+                        out=bank[:, t, :],
+                        lhsT=w1_codes[z][:, rows].bitcast(FP8X4),
+                        lhsT_scale=w1_plane[z][:, rows],
+                        rhs=x_codes[z][:, cols].bitcast(FP8X4),
+                        rhs_scale=x_plane[4 * z : P, cols],
+                        start=(z == 0),
+                        stop=(z == PASSES - 1),
+                    )
+            h = keep.tile([P, CHUNK, PACK], BF16, name="h", tag="h_%d" % c, align_bytes=64)
+            nc.scalar.activation(h[:], bank[:].rearrange("p t n -> p n t"), GELU)
+            codes = keep.tile([P, CHUNK], U32, name="h_codes_%d" % c, align_bytes=64)
+            plane = keep.tile([P, CHUNK], U8, name="h_plane_%d" % c, align_bytes=64)
+            nc.vector.quantize_mx(
+                out=codes[:].bitcast(FP8X4), scales=plane[:], in_=h[:].rearrange("p n t -> p (n t)")
+            )
+            h_mx[c] = (codes, plane)
+
+        def put(b, first, last, update, old):
+            nc.vector.tensor_tensor(stream[b][:].indirect(entries(first, last)), update, old, ADD)
+
+        def second_direct():
+            codes, plane = h_mx[0]
+            y_bank = psum.tile([P, CHUNK], F32, name="y_first")
+            nc.tensor.matmul_mx(
+                out=y_bank[:],
+                lhsT=w2_codes[:, 0:P].bitcast(FP8X4),
+                lhsT_scale=w2_plane[:, 0:P],
+                rhs=codes[:].bitcast(FP8X4),
+                rhs_scale=plane[:],
+                start=True,
+                stop=True,
+            )
+            update = keep.tile([P, CHUNK], F32, name="update_first", align_bytes=64)
+            nc.vector.tensor_tensor(update[:], y_bank[:], gate_first[:], MULT)
+            put(0, 0, CHUNK, update[:], old_upper[:, 0:CHUNK])
+
+        def gated_rows(c, first):
+            codes, plane = h_mx[c]
+            y_bank = psum.tile([P, N - first], F32, name="y_bank", tag=y_tags[c])
+            nc.tensor.matmul_mx(
+                out=y_bank[:],
+                lhsT=codes[:].bitcast(FP8X4),
+                lhsT_scale=plane[:],
+                rhs=w2_codes[:, first:N].bitcast(FP8X4),
+                rhs_scale=w2_plane[:, first:N],
+                start=True,
+                stop=True,
+            )
+            gated = keep.tile([P, N - first], F32, name="gated_%d" % c)
+            nc.scalar.activation(gated[:], y_bank[:], COPY, scale=gate_cols[:, c : c + 1])
+            return gated
+
+        def turn_back(c, gated, count):
+            turned = psum.tile([P, count, CHUNK], F32, name="turned", tag=turn_tags[c])
+            for b in range(count):
+                nc.tensor.transpose(turned[:, b, :], gated[:, b * P : (b + 1) * P], identity[:])
+            update = keep.tile([P, count, CHUNK], F32, name="update_%d" % c, align_bytes=64)
+            nc.scalar.copy(out=update[:], in_=turned[:])
+            return update
+
+        hidden(0)
+        old_lower_rest = keep.tile([P, S - CHUNK], F32, name="old_lower_rest", tag="h_0", align_bytes=64)
+        nc.vector.tensor_copy(old_lower_rest[:], stream[1][:].indirect(entries(CHUNK, S)))
+        hidden(1)
+        second_direct()
+        hidden(2)
+        hidden(3)
+        update = turn_back(0, gated_rows(0, P), 1)
+        put(1, 0, CHUNK, update[:, 0, :], old_lower_first[:])
+        update = turn_back(1, gated_rows(1, 0), 2)
+        put(0, CHUNK, 2 * CHUNK, update[:, 0, :], old_upper[:, CHUNK : 2 * CHUNK])
+        put(1, CHUNK, 2 * CHUNK, update[:, 1, :], old_lower_rest[:, 0:CHUNK])
+        for c in range(2, CHUNKS):
+            gated = gated_rows(c, 0)
+            update = turn_back(c, gated, 1)
+            nc.tensor.transpose(turned_last[:, (c - 2) * CHUNK : (c - 1) * CHUNK], gated[:, P:N], identity[:])
+            put(0, c * CHUNK, (c + 1) * CHUNK, update[:, 0, :], old_upper[:, c * CHUNK : (c + 1) * CHUNK])
+        nc.sync.dma_start(out=out[0:P, :], in_=stream[0][:])
+        update_last = keep.tile([P, 2 * CHUNK], F32, name="update_last", align_bytes=64)
+        nc.scalar.copy(out=update_last[:], in_=turned_last[:])
+        put(1, 2 * CHUNK, S, update_last[:], old_lower_rest[:, CHUNK : S - CHUNK])
+        nc.sync.dma_start(out=out[P : 2 * P, :], in_=stream[1][:])

@@ -41,31 +41,24 @@ def tile_picked_modres_mlpgelu_p_kernel(tc, x_words, x_scales, gate, res, w1, w2
             return offsets[:, first // LIST_ROWS : last // LIST_ROWS]
 
         xs_window = keep.tile([P, T], U8, name="xs_window", align_bytes=64)
-        warm_in = keep.tile([P, 8], F32, name="warm_in")
-        warm_out = keep.tile([P, 8], F32, name="warm_out")
         identity = keep.tile([P, P], F32, name="identity")
         nc.vector.memset(xs_window[:].bitcast(I32), 0)
-        nc.vector.memset(warm_in[:], 0.0)
-        nc.scalar.activation(warm_out[:], warm_in[:], GELU)
         make_identity(nc, identity[:])
 
-        w1_raw = {}
-
-        def load_w1(z, half):
-            raw = keep.tile([P, PACK, HALF], F32, name="w1_raw_%d_%d" % (z, half), align_bytes=64)
-            rows = w1[z * K_PASS : (z + 1) * K_PASS, half * HALF : (half + 1) * HALF]
+        def load_w1(name, z, first, last):
+            raw = keep.tile([P, PACK, last - first], F32, name=name, align_bytes=64)
+            rows = w1[z * K_PASS : (z + 1) * K_PASS, first:last]
             nc.sync.dma_start(out=raw[:], in_=rows.rearrange("(p j) c -> p j c", j=PACK))
-            w1_raw[z, half] = raw
+            return raw
 
         nc.sync.dma_start(offsets[:], offs)
-        load_w1(0, 0)
+        w1_first = load_w1("w1_first", 0, 0, H)
         for q in range(4):
             nc.sync.dma_start(
                 out=xs_window[32 * q : 32 * q + 4 * PASSES, :].bitcast(I32),
                 in_=x_scales[:, 4 * q : 4 * q + 4, :].bitcast(I32),
             )
-        load_w1(0, 1)
-        load_w1(1, 0)
+        w1_left = load_w1("w1_left", 1, 0, HALF)
         x_window = []
         for z in range(PASSES):
             window = keep.tile([P, T], U32, name="x_window_%d" % z, align_bytes=64)
@@ -74,7 +67,7 @@ def tile_picked_modres_mlpgelu_p_kernel(tc, x_words, x_scales, gate, res, w1, w2
                 in_=x_words[z].rearrange("p n t -> p (n t)").bitcast(I32),
             )
             x_window.append(window)
-        load_w1(1, 1)
+        w1_right = load_w1("w1_right", 1, HALF, H)
         stream = [keep.tile([P, T], F32, name="stream_%d" % b, align_bytes=64) for b in range(BLOCKS)]
         for b in range(BLOCKS):
             nc.sync.dma_start(out=stream[b][:], in_=res[b * P : (b + 1) * P, :])
@@ -86,9 +79,11 @@ def tile_picked_modres_mlpgelu_p_kernel(tc, x_words, x_scales, gate, res, w1, w2
         w1_codes = [keep.tile([P, H], U32, name="w1_codes_%d" % z, align_bytes=64) for z in range(PASSES)]
         w1_plane = [keep.tile([P, H], U8, name="w1_plane_%d" % z, align_bytes=64) for z in range(PASSES)]
 
-        def round_w1(copy, z, half, t0, t1):
-            dst = grouped[z][:, t0:t1, half * 64 : (half + 1) * 64, :].rearrange("p t m j -> p m j t")
-            src = w1_raw[z, half][:].rearrange("p j (m t) -> p m j t", t=PACK)[:, :, :, t0:t1]
+        def round_w1(copy, raw, z, first, pair):
+            count = raw.shape[2] // PACK
+            ts = slice(2 * pair, 2 * pair + 2)
+            dst = grouped[z][:, ts, first : first + count, :].rearrange("p t m j -> p m j t")
+            src = raw[:].rearrange("p j (m t) -> p m j t", t=PACK)[:, :, :, ts]
             copy(out=dst, in_=src)
 
         def quantize_w1(z, t0, t1):
@@ -98,31 +93,32 @@ def tile_picked_modres_mlpgelu_p_kernel(tc, x_words, x_scales, gate, res, w1, w2
                 in_=grouped[z][:, t0:t1, :, :].rearrange("p t m j -> p (t m j)"),
             )
 
-        round_w1(nc.scalar.copy, 0, 0, 0, PACK)
-        round_w1(nc.scalar.copy, 0, 1, 0, PACK)
+        round_w1(nc.vector.tensor_copy, w1_first, 0, 0, 0)
+        round_w1(nc.scalar.copy, w1_first, 0, 0, 1)
         quantize_w1(0, 0, PACK)
-        round_w1(nc.scalar.copy, 1, 0, 0, PACK)
+        for pair in range(2):
+            round_w1(nc.scalar.copy, w1_left, 1, 0, pair)
 
         x_codes = [keep.tile([P, S], U32, name="x_codes_%d" % z, align_bytes=64) for z in range(PASSES)]
         for z in range(PASSES):
             nc.vector.tensor_copy(x_codes[z][:], x_window[z][:].indirect(offsets[:]))
 
-        round_w1(nc.vector.tensor_copy, 1, 1, 0, 2)
-        round_w1(nc.scalar.copy, 1, 1, 2, PACK)
+        round_w1(nc.vector.tensor_copy, w1_right, 1, P // 2, 0)
+        round_w1(nc.scalar.copy, w1_right, 1, P // 2, 1)
         quantize_w1(1, 0, 2)
         quantize_w1(1, 2, PACK)
 
-        w2_plane = keep.tile([P, N], U8, name="w2_plane", tag="w1_raw_0_0", align_bytes=64)
+        w2_plane = keep.tile([P, N], U8, name="w2_plane", tag="w1_first", align_bytes=64)
         nc.gpsimd.memset(w2_plane[:].bitcast(I32), 0)
         for q in range(4):
             nc.scalar.dma_start(
                 out=w2_plane[32 * q : 32 * q + 4, :].bitcast(I32),
                 in_=w2_scales[0, 4 * q : 4 * q + 4, :].bitcast(I32),
             )
-        gate_rows = keep.tile([P, P], F32, name="gate_rows", tag="w1_raw_0_1", align_bytes=64)
+        gate_rows = keep.tile([P, P], F32, name="gate_rows", tag="xs_window", align_bytes=64)
         nc.gpsimd.memset(gate_rows[:], 0.0)
         nc.scalar.dma_start(out=gate_rows[0:CHUNKS, :], in_=gate[0].rearrange("(c p) -> c p", p=P))
-        gate_first = keep.tile([P, CHUNK], F32, name="gate_first", tag="w1_raw_1_0", align_bytes=64)
+        gate_first = keep.tile([P, CHUNK], F32, name="gate_first", tag="w1_left", align_bytes=64)
         nc.scalar.dma_start(out=gate_first[:], in_=gate[:, 0:CHUNK])
         w2_codes = keep.tile([P, N], U32, name="w2_codes", tag="x_window_0", align_bytes=64)
         nc.scalar.dma_start(
@@ -136,11 +132,11 @@ def tile_picked_modres_mlpgelu_p_kernel(tc, x_words, x_scales, gate, res, w1, w2
 
         old_upper = keep.tile([P, S], F32, name="old_upper", align_bytes=64)
         nc.vector.tensor_copy(old_upper[:], stream[0][:].indirect(offsets[:]))
-        old_lower_first = keep.tile([P, CHUNK], F32, name="old_lower_first", align_bytes=64)
-        nc.vector.tensor_copy(old_lower_first[:], stream[1][:].indirect(entries(0, CHUNK)))
+        old_lower_first = keep.tile([P, 2 * CHUNK], F32, name="old_lower_first", align_bytes=64)
+        nc.vector.tensor_copy(old_lower_first[:], stream[1][:].indirect(entries(0, 2 * CHUNK)))
 
         turned_last = psum.tile([P, 2 * CHUNK], F32, name="turned_last")
-        h_tags = ["h_a", "h_b", "h_c", "h_b"]
+        h_tags = ["h_a", "h_b", "h_c", "y_first"]
         y_tags = ["y_even", "y_odd", "y_even", "y_odd"]
         turn_tags = ["h_a", "turn_odd", "h_a", "turn_odd"]
         h_mx = {}
@@ -213,17 +209,17 @@ def tile_picked_modres_mlpgelu_p_kernel(tc, x_words, x_scales, gate, res, w1, w2
             return update
 
         hidden(0)
-        old_lower_rest = keep.tile([P, S - CHUNK], F32, name="old_lower_rest", tag="h_0", align_bytes=64)
-        nc.vector.tensor_copy(old_lower_rest[:], stream[1][:].indirect(entries(CHUNK, S)))
+        old_lower_rest = keep.tile([P, 2 * CHUNK], F32, name="old_lower_rest", tag="h_0", align_bytes=64)
+        nc.vector.tensor_copy(old_lower_rest[:], stream[1][:].indirect(entries(2 * CHUNK, S)))
         hidden(1)
         second_direct()
+        update = turn_back(0, gated_rows(0, P), 1)
         hidden(2)
         hidden(3)
-        update = turn_back(0, gated_rows(0, P), 1)
-        put(1, 0, CHUNK, update[:, 0, :], old_lower_first[:])
+        put(1, 0, CHUNK, update[:, 0, :], old_lower_first[:, 0:CHUNK])
         update = turn_back(1, gated_rows(1, 0), 2)
         put(0, CHUNK, 2 * CHUNK, update[:, 0, :], old_upper[:, CHUNK : 2 * CHUNK])
-        put(1, CHUNK, 2 * CHUNK, update[:, 1, :], old_lower_rest[:, 0:CHUNK])
+        put(1, CHUNK, 2 * CHUNK, update[:, 1, :], old_lower_first[:, CHUNK : 2 * CHUNK])
         for c in range(2, CHUNKS):
             gated = gated_rows(c, 0)
             update = turn_back(c, gated, 1)
@@ -232,5 +228,5 @@ def tile_picked_modres_mlpgelu_p_kernel(tc, x_words, x_scales, gate, res, w1, w2
         nc.sync.dma_start(out=out[0:P, :], in_=stream[0][:])
         update_last = keep.tile([P, 2 * CHUNK], F32, name="update_last", align_bytes=64)
         nc.scalar.copy(out=update_last[:], in_=turned_last[:])
-        put(1, 2 * CHUNK, S, update_last[:], old_lower_rest[:, CHUNK : S - CHUNK])
+        put(1, 2 * CHUNK, S, update_last[:], old_lower_rest[:])
         nc.sync.dma_start(out=out[P : 2 * P, :], in_=stream[1][:])

@@ -43,6 +43,14 @@ def tile_picked_modres_mlpgelu_p_kernel(tc, x_words, x_scales, gate, res, w1, w2
         xs_window = keep.tile([P, T], U8, name="xs_window", align_bytes=64)
         identity = keep.tile([P, P], F32, name="identity")
         nc.vector.memset(xs_window[:].bitcast(I32), 0)
+        warm_in = keep.tile([P, 8], F32, name="warm_in")
+        warm_out = keep.tile([P, 8], F32, name="warm_out")
+        nc.vector.memset(warm_in[:], 0.0)
+        nc.scalar.activation(warm_out[:], warm_in[:], GELU)
+        w2_plane = keep.tile([P, N], U8, name="w2_plane", align_bytes=64)
+        nc.gpsimd.memset(w2_plane[:].bitcast(I32), 0)
+        gate_rows = keep.tile([P, P], F32, name="gate_rows", align_bytes=64)
+        nc.gpsimd.memset(gate_rows[:], 0.0)
         make_identity(nc, identity[:])
 
         def load_w1(name, z, first, last):
@@ -52,21 +60,35 @@ def tile_picked_modres_mlpgelu_p_kernel(tc, x_words, x_scales, gate, res, w1, w2
             return raw
 
         nc.sync.dma_start(offsets[:], offs)
-        w1_first = load_w1("w1_first", 0, 0, H)
-        for q in range(4):
-            nc.sync.dma_start(
-                out=xs_window[32 * q : 32 * q + 4 * PASSES, :].bitcast(I32),
-                in_=x_scales[:, 4 * q : 4 * q + 4, :].bitcast(I32),
-            )
-        w1_left = load_w1("w1_left", 1, 0, HALF)
-        x_window = []
-        for z in range(PASSES):
+
+        def load_x(z):
             window = keep.tile([P, T], U32, name="x_window_%d" % z, align_bytes=64)
             nc.sync.dma_start(
                 out=window[:].bitcast(I32),
                 in_=x_words[z].rearrange("p n t -> p (n t)").bitcast(I32),
             )
-            x_window.append(window)
+            return window
+
+        x_window = [load_x(0)]
+        w2_codes = keep.tile([P, N], U32, name="w2_codes", align_bytes=64)
+        nc.sync.dma_start(
+            out=w2_codes[:].bitcast(I32),
+            in_=w2_words[0].rearrange("p n t -> p (n t)").bitcast(I32),
+        )
+        for q in range(4):
+            nc.sync.dma_start(
+                out=xs_window[32 * q : 32 * q + 4 * PASSES, :].bitcast(I32),
+                in_=x_scales[:, 4 * q : 4 * q + 4, :].bitcast(I32),
+            )
+        w1_first = load_w1("w1_first", 0, 0, H)
+        w1_left = load_w1("w1_left", 1, 0, HALF)
+        for q in range(4):
+            nc.sync.dma_start(
+                out=w2_plane[32 * q : 32 * q + 4, :].bitcast(I32),
+                in_=w2_scales[0, 4 * q : 4 * q + 4, :].bitcast(I32),
+            )
+        nc.sync.dma_start(out=gate_rows[0:CHUNKS, :], in_=gate[0].rearrange("(c p) -> c p", p=P))
+        x_window.append(load_x(1))
         w1_right = load_w1("w1_right", 1, HALF, H)
         stream = [keep.tile([P, T], F32, name="stream_%d" % b, align_bytes=64) for b in range(BLOCKS)]
         for b in range(BLOCKS):
@@ -108,23 +130,8 @@ def tile_picked_modres_mlpgelu_p_kernel(tc, x_words, x_scales, gate, res, w1, w2
         quantize_w1(1, 0, 2)
         quantize_w1(1, 2, PACK)
 
-        w2_plane = keep.tile([P, N], U8, name="w2_plane", tag="w1_first", align_bytes=64)
-        nc.gpsimd.memset(w2_plane[:].bitcast(I32), 0)
-        for q in range(4):
-            nc.scalar.dma_start(
-                out=w2_plane[32 * q : 32 * q + 4, :].bitcast(I32),
-                in_=w2_scales[0, 4 * q : 4 * q + 4, :].bitcast(I32),
-            )
-        gate_rows = keep.tile([P, P], F32, name="gate_rows", tag="xs_window", align_bytes=64)
-        nc.gpsimd.memset(gate_rows[:], 0.0)
-        nc.scalar.dma_start(out=gate_rows[0:CHUNKS, :], in_=gate[0].rearrange("(c p) -> c p", p=P))
-        gate_first = keep.tile([P, CHUNK], F32, name="gate_first", tag="w1_left", align_bytes=64)
+        gate_first = keep.tile([P, CHUNK], F32, name="gate_first", tag="x_window_1", align_bytes=64)
         nc.scalar.dma_start(out=gate_first[:], in_=gate[:, 0:CHUNK])
-        w2_codes = keep.tile([P, N], U32, name="w2_codes", tag="x_window_0", align_bytes=64)
-        nc.scalar.dma_start(
-            out=w2_codes[:].bitcast(I32),
-            in_=w2_words[0].rearrange("p n t -> p (n t)").bitcast(I32),
-        )
         gate_bank = psum.tile([P, P], F32, name="gate_bank", tag="turn_odd")
         nc.tensor.transpose(gate_bank[:], gate_rows[:], identity[:])
         gate_cols = keep.tile([P, CHUNKS], F32, name="gate_cols")
@@ -132,11 +139,9 @@ def tile_picked_modres_mlpgelu_p_kernel(tc, x_words, x_scales, gate, res, w1, w2
 
         old_upper = keep.tile([P, S], F32, name="old_upper", align_bytes=64)
         nc.vector.tensor_copy(old_upper[:], stream[0][:].indirect(offsets[:]))
-        old_lower_first = keep.tile([P, 2 * CHUNK], F32, name="old_lower_first", align_bytes=64)
-        nc.vector.tensor_copy(old_lower_first[:], stream[1][:].indirect(entries(0, 2 * CHUNK)))
 
         turned_last = psum.tile([P, 2 * CHUNK], F32, name="turned_last")
-        h_tags = ["h_a", "h_b", "h_c", "y_first"]
+        h_tags = ["h_a", "h_b", "h_c", "h_b"]
         y_tags = ["y_even", "y_odd", "y_even", "y_odd"]
         turn_tags = ["h_a", "turn_odd", "h_a", "turn_odd"]
         h_mx = {}
@@ -209,10 +214,12 @@ def tile_picked_modres_mlpgelu_p_kernel(tc, x_words, x_scales, gate, res, w1, w2
             return update
 
         hidden(0)
-        old_lower_rest = keep.tile([P, 2 * CHUNK], F32, name="old_lower_rest", tag="h_0", align_bytes=64)
-        nc.vector.tensor_copy(old_lower_rest[:], stream[1][:].indirect(entries(2 * CHUNK, S)))
+        old_lower_first = keep.tile([P, 2 * CHUNK], F32, name="old_lower_first", tag="h_0", align_bytes=64)
+        nc.vector.tensor_copy(old_lower_first[:], stream[1][:].indirect(entries(0, 2 * CHUNK)))
         hidden(1)
         second_direct()
+        old_lower_rest = keep.tile([P, 2 * CHUNK], F32, name="old_lower_rest", tag="h_1", align_bytes=64)
+        nc.vector.tensor_copy(old_lower_rest[:], stream[1][:].indirect(entries(2 * CHUNK, S)))
         update = turn_back(0, gated_rows(0, P), 1)
         hidden(2)
         hidden(3)

@@ -49,8 +49,6 @@ def tile_picked_modres_mlpgelu_p_kernel(tc, x_words, x_scales, gate, res, w1, w2
         nc.scalar.activation(warm_out[:], warm_in[:], GELU)
         w2_plane = keep.tile([P, N], U8, name="w2_plane", align_bytes=64)
         nc.gpsimd.memset(w2_plane[:].bitcast(I32), 0)
-        gate_rows = keep.tile([P, P], F32, name="gate_rows", align_bytes=64)
-        nc.gpsimd.memset(gate_rows[:], 0.0)
         make_identity(nc, identity[:])
 
         def load_w1(name, z, first, last):
@@ -70,11 +68,6 @@ def tile_picked_modres_mlpgelu_p_kernel(tc, x_words, x_scales, gate, res, w1, w2
             return window
 
         x_window = [load_x(0)]
-        w2_codes = keep.tile([P, N], U32, name="w2_codes", align_bytes=64)
-        nc.sync.dma_start(
-            out=w2_codes[:].bitcast(I32),
-            in_=w2_words[0].rearrange("p n t -> p (n t)").bitcast(I32),
-        )
         for q in range(4):
             nc.sync.dma_start(
                 out=xs_window[32 * q : 32 * q + 4 * PASSES, :].bitcast(I32),
@@ -87,12 +80,16 @@ def tile_picked_modres_mlpgelu_p_kernel(tc, x_words, x_scales, gate, res, w1, w2
                 out=w2_plane[32 * q : 32 * q + 4, :].bitcast(I32),
                 in_=w2_scales[0, 4 * q : 4 * q + 4, :].bitcast(I32),
             )
-        nc.sync.dma_start(out=gate_rows[0:CHUNKS, :], in_=gate[0].rearrange("(c p) -> c p", p=P))
-        x_window.append(load_x(1))
         w1_right = load_w1("w1_right", 1, HALF, H)
+        x_window.append(load_x(1))
         stream = [keep.tile([P, T], F32, name="stream_%d" % b, align_bytes=64) for b in range(BLOCKS)]
         for b in range(BLOCKS):
             nc.sync.dma_start(out=stream[b][:], in_=res[b * P : (b + 1) * P, :])
+        w2_codes = keep.tile([P, N], U32, name="w2_codes", align_bytes=64)
+        nc.sync.dma_start(
+            out=w2_codes[:].bitcast(I32),
+            in_=w2_words[0].rearrange("p n t -> p (n t)").bitcast(I32),
+        )
 
         x_plane = keep.tile([P, S], U8, name="x_plane", align_bytes=64)
         nc.vector.tensor_copy(x_plane[:], xs_window[:].indirect(offsets[:]))
@@ -122,18 +119,25 @@ def tile_picked_modres_mlpgelu_p_kernel(tc, x_words, x_scales, gate, res, w1, w2
             round_w1(nc.scalar.copy, w1_left, 1, 0, pair)
 
         x_codes = [keep.tile([P, S], U32, name="x_codes_%d" % z, align_bytes=64) for z in range(PASSES)]
-        for z in range(PASSES):
-            nc.vector.tensor_copy(x_codes[z][:], x_window[z][:].indirect(offsets[:]))
+        nc.vector.tensor_copy(x_codes[0][:], x_window[0][:].indirect(offsets[:]))
 
         round_w1(nc.vector.tensor_copy, w1_right, 1, P // 2, 0)
         round_w1(nc.scalar.copy, w1_right, 1, P // 2, 1)
         quantize_w1(1, 0, 2)
         quantize_w1(1, 2, PACK)
 
-        gate_first = keep.tile([P, CHUNK], F32, name="gate_first", tag="x_window_1", align_bytes=64)
-        nc.scalar.dma_start(out=gate_first[:], in_=gate[:, 0:CHUNK])
+        nc.vector.tensor_copy(x_codes[1][:, 0:CHUNK], x_window[1][:].indirect(entries(0, CHUNK)))
+        nc.vector.tensor_copy(x_codes[1][:, CHUNK:S], x_window[1][:].indirect(entries(CHUNK, S)))
+
+        gates = keep.tile([P, 2 * CHUNK], F32, name="gates", tag="x_window_1", align_bytes=64)
+        gate_first = gates[:, 0:CHUNK]
+        gate_rows = gates[:, CHUNK : 2 * CHUNK]
+        nc.gpsimd.memset(gate_rows, 0.0)
+        for first in range(0, CHUNK, CHUNK // 2):
+            nc.scalar.dma_start(out=gates[:, first : first + CHUNK // 2], in_=gate[:, first : first + CHUNK // 2])
+        nc.scalar.dma_start(out=gates[0:CHUNKS, CHUNK : 2 * CHUNK], in_=gate[0].rearrange("(c p) -> c p", p=P))
         gate_bank = psum.tile([P, P], F32, name="gate_bank", tag="turn_odd")
-        nc.tensor.transpose(gate_bank[:], gate_rows[:], identity[:])
+        nc.tensor.transpose(gate_bank[:], gate_rows, identity[:])
         gate_cols = keep.tile([P, CHUNKS], F32, name="gate_cols")
         nc.scalar.copy(out=gate_cols[:], in_=gate_bank[:, 0:CHUNKS])
 
@@ -186,7 +190,7 @@ def tile_picked_modres_mlpgelu_p_kernel(tc, x_words, x_scales, gate, res, w1, w2
                 stop=True,
             )
             update = keep.tile([P, CHUNK], F32, name="update_first", align_bytes=64)
-            nc.vector.tensor_tensor(update[:], y_bank[:], gate_first[:], MULT)
+            nc.vector.tensor_tensor(update[:], y_bank[:], gate_first, MULT)
             put(0, 0, CHUNK, update[:], old_upper[:, 0:CHUNK])
 
         def gated_rows(c, first):
@@ -213,13 +217,13 @@ def tile_picked_modres_mlpgelu_p_kernel(tc, x_words, x_scales, gate, res, w1, w2
             nc.scalar.copy(out=update[:], in_=turned[:])
             return update
 
-        hidden(0)
-        old_lower_first = keep.tile([P, 2 * CHUNK], F32, name="old_lower_first", tag="h_0", align_bytes=64)
+        old_lower_first = keep.tile([P, 2 * CHUNK], F32, name="old_lower_first", align_bytes=64)
         nc.vector.tensor_copy(old_lower_first[:], stream[1][:].indirect(entries(0, 2 * CHUNK)))
+        hidden(0)
+        old_lower_rest = keep.tile([P, 2 * CHUNK], F32, name="old_lower_rest", tag="h_0", align_bytes=64)
+        nc.vector.tensor_copy(old_lower_rest[:], stream[1][:].indirect(entries(2 * CHUNK, S)))
         hidden(1)
         second_direct()
-        old_lower_rest = keep.tile([P, 2 * CHUNK], F32, name="old_lower_rest", tag="h_1", align_bytes=64)
-        nc.vector.tensor_copy(old_lower_rest[:], stream[1][:].indirect(entries(2 * CHUNK, S)))
         update = turn_back(0, gated_rows(0, P), 1)
         hidden(2)
         hidden(3)
@@ -227,11 +231,15 @@ def tile_picked_modres_mlpgelu_p_kernel(tc, x_words, x_scales, gate, res, w1, w2
         update = turn_back(1, gated_rows(1, 0), 2)
         put(0, CHUNK, 2 * CHUNK, update[:, 0, :], old_upper[:, CHUNK : 2 * CHUNK])
         put(1, CHUNK, 2 * CHUNK, update[:, 1, :], old_lower_first[:, CHUNK : 2 * CHUNK])
+        turned_upper = psum.tile([P, 2 * CHUNK], F32, name="turned_upper", tag="h_a")
         for c in range(2, CHUNKS):
             gated = gated_rows(c, 0)
-            update = turn_back(c, gated, 1)
-            nc.tensor.transpose(turned_last[:, (c - 2) * CHUNK : (c - 1) * CHUNK], gated[:, P:N], identity[:])
-            put(0, c * CHUNK, (c + 1) * CHUNK, update[:, 0, :], old_upper[:, c * CHUNK : (c + 1) * CHUNK])
+            cols = slice((c - 2) * CHUNK, (c - 1) * CHUNK)
+            nc.tensor.transpose(turned_upper[:, cols], gated[:, 0:P], identity[:])
+            nc.tensor.transpose(turned_last[:, cols], gated[:, P:N], identity[:])
+        update_upper = keep.tile([P, 2 * CHUNK], F32, name="update_upper", align_bytes=64)
+        nc.scalar.copy(out=update_upper[:], in_=turned_upper[:])
+        put(0, 2 * CHUNK, S, update_upper[:], old_upper[:, 2 * CHUNK : S])
         nc.sync.dma_start(out=out[0:P, :], in_=stream[0][:])
         update_last = keep.tile([P, 2 * CHUNK], F32, name="update_last", align_bytes=64)
         nc.scalar.copy(out=update_last[:], in_=turned_last[:])

@@ -22,14 +22,20 @@ P = 128
 PACK = 4
 K_PASS = P * PACK
 PASSES = K // K_PASS
+QUADRANTS, QUADRANT = 4, 32
+SCALE_ROWS = 4
+LIST_ROWS = 16
 CHUNK = 128
 CHUNKS = S // CHUNK
-BLOCKS = N // P
-HALF = H // 2
-LIST_ROWS = 16
+HALF_LIST = S // 2
+HALF_H = H // 2
+UPPER, LOWER = 0, 1
+ALIGN = 64
 
 
-def tile_picked_modres_mlpgelu_p_kernel(tc, x_words, x_scales, gate, res, w1, w2_words, w2_scales, offs, out):
+def tile_picked_modres_mlpgelu_p_kernel(
+    tc, x_words, x_scales, gate, res, w1, w2_words, w2_scales, offs, out
+):
     nc = tc.nc
     with ExitStack() as ctx:
         keep = ctx.enter_context(tc.tile_pool(name="keep", bufs=1))
@@ -40,76 +46,73 @@ def tile_picked_modres_mlpgelu_p_kernel(tc, x_words, x_scales, gate, res, w1, w2
         def entries(first, last):
             return offsets[:, first // LIST_ROWS : last // LIST_ROWS]
 
-        xs_window = keep.tile([P, T], U8, name="xs_window", align_bytes=64)
+        x_scale_window = keep.tile([P, T], U8, name="x_scale_window", align_bytes=ALIGN)
         identity = keep.tile([P, P], F32, name="identity")
-        nc.vector.memset(xs_window[:].bitcast(I32), 0)
-        warm_in = keep.tile([P, 8], F32, name="warm_in")
-        warm_out = keep.tile([P, 8], F32, name="warm_out")
-        nc.vector.memset(warm_in[:], 0.0)
-        nc.scalar.activation(warm_out[:], warm_in[:], GELU)
-        w2_plane = keep.tile([P, N], U8, name="w2_plane", align_bytes=64)
+        nc.vector.memset(x_scale_window[:].bitcast(I32), 0)
+        w2_plane = keep.tile([P, N], U8, name="w2_plane", align_bytes=ALIGN)
         nc.gpsimd.memset(w2_plane[:].bitcast(I32), 0)
         make_identity(nc, identity[:])
 
         def load_w1(name, z, first, last):
-            raw = keep.tile([P, PACK, last - first], F32, name=name, align_bytes=64)
+            raw = keep.tile([P, PACK, last - first], F32, name=name, align_bytes=ALIGN)
             rows = w1[z * K_PASS : (z + 1) * K_PASS, first:last]
             nc.sync.dma_start(out=raw[:], in_=rows.rearrange("(p j) c -> p j c", j=PACK))
             return raw
 
-        nc.sync.dma_start(offsets[:], offs)
-
         def load_x(z):
-            window = keep.tile([P, T], U32, name="x_window_%d" % z, align_bytes=64)
+            window = keep.tile([P, T], U32, name="x_window_%d" % z, align_bytes=ALIGN)
             nc.sync.dma_start(
                 out=window[:].bitcast(I32),
-                in_=x_words[z].rearrange("p n t -> p (n t)").bitcast(I32),
+                in_=x_words[z].rearrange("p n r -> p (n r)").bitcast(I32),
             )
             return window
 
+        nc.sync.dma_start(offsets[:], offs)
         x_window = [load_x(0)]
-        for q in range(4):
+        for q in range(QUADRANTS):
             nc.sync.dma_start(
-                out=xs_window[32 * q : 32 * q + 4 * PASSES, :].bitcast(I32),
-                in_=x_scales[:, 4 * q : 4 * q + 4, :].bitcast(I32),
+                out=x_scale_window[QUADRANT * q : QUADRANT * q + SCALE_ROWS * PASSES, :].bitcast(I32),
+                in_=x_scales[:, SCALE_ROWS * q : SCALE_ROWS * (q + 1), :].bitcast(I32),
             )
         w1_first = load_w1("w1_first", 0, 0, H)
-        w1_left = load_w1("w1_left", 1, 0, HALF)
-        for q in range(4):
+        w1_left = load_w1("w1_left", 1, 0, HALF_H)
+        for q in range(QUADRANTS):
             nc.sync.dma_start(
-                out=w2_plane[32 * q : 32 * q + 4, :].bitcast(I32),
-                in_=w2_scales[0, 4 * q : 4 * q + 4, :].bitcast(I32),
+                out=w2_plane[QUADRANT * q : QUADRANT * q + SCALE_ROWS, :].bitcast(I32),
+                in_=w2_scales[0, SCALE_ROWS * q : SCALE_ROWS * (q + 1), :].bitcast(I32),
             )
-        w1_right = load_w1("w1_right", 1, HALF, H)
+        w1_right = load_w1("w1_right", 1, HALF_H, H)
         x_window.append(load_x(1))
-        stream = [keep.tile([P, T], F32, name="stream_%d" % b, align_bytes=64) for b in range(BLOCKS)]
-        for b in range(BLOCKS):
+        stream = [keep.tile([P, T], F32, name="stream_%d" % b, align_bytes=ALIGN) for b in (UPPER, LOWER)]
+        for b in (UPPER, LOWER):
             nc.sync.dma_start(out=stream[b][:], in_=res[b * P : (b + 1) * P, :])
-        w2_codes = keep.tile([P, N], U32, name="w2_codes", align_bytes=64)
+        w2_codes = keep.tile([P, N], U32, name="w2_codes", align_bytes=ALIGN)
         nc.sync.dma_start(
             out=w2_codes[:].bitcast(I32),
-            in_=w2_words[0].rearrange("p n t -> p (n t)").bitcast(I32),
+            in_=w2_words[0].rearrange("p n r -> p (n r)").bitcast(I32),
         )
 
-        x_plane = keep.tile([P, S], U8, name="x_plane", align_bytes=64)
-        nc.vector.tensor_copy(x_plane[:], xs_window[:].indirect(offsets[:]))
+        x_plane = keep.tile([P, S], U8, name="x_plane", align_bytes=ALIGN)
+        nc.vector.tensor_copy(x_plane[:], x_scale_window[:].indirect(offsets[:]))
 
-        grouped = [keep.tile([P, PACK, P, PACK], BF16, name="w1_grouped_%d" % z, align_bytes=64) for z in range(PASSES)]
-        w1_codes = [keep.tile([P, H], U32, name="w1_codes_%d" % z, align_bytes=64) for z in range(PASSES)]
-        w1_plane = [keep.tile([P, H], U8, name="w1_plane_%d" % z, align_bytes=64) for z in range(PASSES)]
+        grouped = [
+            keep.tile([P, PACK, P, PACK], BF16, name="w1_grouped_%d" % z, align_bytes=ALIGN) for z in range(PASSES)
+        ]
+        w1_codes = [keep.tile([P, H], U32, name="w1_codes_%d" % z, align_bytes=ALIGN) for z in range(PASSES)]
+        w1_plane = [keep.tile([P, H], U8, name="w1_plane_%d" % z, align_bytes=ALIGN) for z in range(PASSES)]
 
-        def round_w1(copy, raw, z, first, pair):
+        def round_w1(copy, raw, z, first_m, pair):
             count = raw.shape[2] // PACK
             ts = slice(2 * pair, 2 * pair + 2)
-            dst = grouped[z][:, ts, first : first + count, :].rearrange("p t m j -> p m j t")
+            dst = grouped[z][:, ts, first_m : first_m + count, :].rearrange("p t m j -> p m j t")
             src = raw[:].rearrange("p j (m t) -> p m j t", t=PACK)[:, :, :, ts]
             copy(out=dst, in_=src)
 
-        def quantize_w1(z, t0, t1):
+        def quantize_w1(z, first_t, last_t):
             nc.vector.quantize_mx(
-                out=w1_codes[z][:, t0 * P : t1 * P].bitcast(FP8X4),
-                scales=w1_plane[z][:, t0 * P : t1 * P],
-                in_=grouped[z][:, t0:t1, :, :].rearrange("p t m j -> p (t m j)"),
+                out=w1_codes[z][:, first_t * P : last_t * P].bitcast(FP8X4),
+                scales=w1_plane[z][:, first_t * P : last_t * P],
+                in_=grouped[z][:, first_t:last_t, :, :].rearrange("p t m j -> p (t m j)"),
             )
 
         round_w1(nc.vector.tensor_copy, w1_first, 0, 0, 0)
@@ -118,57 +121,55 @@ def tile_picked_modres_mlpgelu_p_kernel(tc, x_words, x_scales, gate, res, w1, w2
         for pair in range(2):
             round_w1(nc.scalar.copy, w1_left, 1, 0, pair)
 
-        x_codes = [keep.tile([P, S], U32, name="x_codes_%d" % z, align_bytes=64) for z in range(PASSES)]
+        x_codes = [keep.tile([P, S], U32, name="x_codes_%d" % z, align_bytes=ALIGN) for z in range(PASSES)]
         nc.vector.tensor_copy(x_codes[0][:], x_window[0][:].indirect(offsets[:]))
 
-        round_w1(nc.vector.tensor_copy, w1_right, 1, P // 2, 0)
-        round_w1(nc.scalar.copy, w1_right, 1, P // 2, 1)
+        round_w1(nc.vector.tensor_copy, w1_right, 1, HALF_H // PACK, 0)
+        round_w1(nc.scalar.copy, w1_right, 1, HALF_H // PACK, 1)
         quantize_w1(1, 0, 2)
         quantize_w1(1, 2, PACK)
 
         nc.vector.tensor_copy(x_codes[1][:, 0:CHUNK], x_window[1][:].indirect(entries(0, CHUNK)))
         nc.vector.tensor_copy(x_codes[1][:, CHUNK:S], x_window[1][:].indirect(entries(CHUNK, S)))
 
-        gates = keep.tile([P, 2 * CHUNK], F32, name="gates", tag="x_window_1", align_bytes=64)
+        gates = keep.tile([P, 2 * CHUNK], F32, name="gates", tag="w1_right", align_bytes=ALIGN)
         gate_first = gates[:, 0:CHUNK]
         gate_rows = gates[:, CHUNK : 2 * CHUNK]
         nc.gpsimd.memset(gate_rows, 0.0)
-        for first in range(0, CHUNK, CHUNK // 2):
-            nc.scalar.dma_start(out=gates[:, first : first + CHUNK // 2], in_=gate[:, first : first + CHUNK // 2])
-        nc.scalar.dma_start(out=gates[0:CHUNKS, CHUNK : 2 * CHUNK], in_=gate[0].rearrange("(c p) -> c p", p=P))
-        gate_bank = psum.tile([P, P], F32, name="gate_bank", tag="turn_odd")
+        nc.scalar.dma_start(out=gate_first, in_=gate[:, 0:CHUNK])
+        nc.scalar.dma_start(out=gates[0:CHUNKS, CHUNK : 2 * CHUNK], in_=gate[0].rearrange("(c j) -> c j", j=CHUNK))
+        gate_bank = psum.tile([P, P], F32, name="gate_bank", tag="turn")
         nc.tensor.transpose(gate_bank[:], gate_rows, identity[:])
         gate_cols = keep.tile([P, CHUNKS], F32, name="gate_cols")
         nc.scalar.copy(out=gate_cols[:], in_=gate_bank[:, 0:CHUNKS])
 
-        old_upper = keep.tile([P, S], F32, name="old_upper", align_bytes=64)
-        nc.vector.tensor_copy(old_upper[:], stream[0][:].indirect(offsets[:]))
+        old_upper = keep.tile([P, S], F32, name="old_upper", align_bytes=ALIGN)
+        nc.vector.tensor_copy(old_upper[:], stream[UPPER][:].indirect(offsets[:]))
 
-        turned_last = psum.tile([P, 2 * CHUNK], F32, name="turned_last")
+        turned_lower = psum.tile([P, HALF_LIST], F32, name="turned_lower")
         h_tags = ["h_a", "h_b", "h_c", "h_b"]
-        y_tags = ["y_even", "y_odd", "y_even", "y_odd"]
-        turn_tags = ["h_a", "turn_odd", "h_a", "turn_odd"]
+        y_tags = ["y_even", "y_odd"]
         h_mx = {}
 
         def hidden(c):
             cols = slice(c * CHUNK, (c + 1) * CHUNK)
             bank = psum.tile([P, PACK, CHUNK], F32, name="h_bank", tag=h_tags[c])
             for t in range(PACK):
-                rows = slice(t * P, (t + 1) * P)
+                units = slice(t * P, (t + 1) * P)
                 for z in range(PASSES):
                     nc.tensor.matmul_mx(
                         out=bank[:, t, :],
-                        lhsT=w1_codes[z][:, rows].bitcast(FP8X4),
-                        lhsT_scale=w1_plane[z][:, rows],
+                        lhsT=w1_codes[z][:, units].bitcast(FP8X4),
+                        lhsT_scale=w1_plane[z][:, units],
                         rhs=x_codes[z][:, cols].bitcast(FP8X4),
-                        rhs_scale=x_plane[4 * z : P, cols],
+                        rhs_scale=x_plane[SCALE_ROWS * z : P, cols],
                         start=(z == 0),
                         stop=(z == PASSES - 1),
                     )
-            h = keep.tile([P, CHUNK, PACK], BF16, name="h", tag="h_%d" % c, align_bytes=64)
+            h = keep.tile([P, CHUNK, PACK], BF16, name="h", tag="h_%d" % c, align_bytes=ALIGN)
             nc.scalar.activation(h[:], bank[:].rearrange("p t n -> p n t"), GELU)
-            codes = keep.tile([P, CHUNK], U32, name="h_codes_%d" % c, align_bytes=64)
-            plane = keep.tile([P, CHUNK], U8, name="h_plane_%d" % c, align_bytes=64)
+            codes = keep.tile([P, CHUNK], U32, name="h_codes_%d" % c, align_bytes=ALIGN)
+            plane = keep.tile([P, CHUNK], U8, name="h_plane_%d" % c, align_bytes=ALIGN)
             nc.vector.quantize_mx(
                 out=codes[:].bitcast(FP8X4), scales=plane[:], in_=h[:].rearrange("p n t -> p (n t)")
             )
@@ -177,7 +178,7 @@ def tile_picked_modres_mlpgelu_p_kernel(tc, x_words, x_scales, gate, res, w1, w2
         def put(b, first, last, update, old):
             nc.vector.tensor_tensor(stream[b][:].indirect(entries(first, last)), update, old, ADD)
 
-        def second_direct():
+        def first_upper_update():
             codes, plane = h_mx[0]
             y_bank = psum.tile([P, CHUNK], F32, name="y_first")
             nc.tensor.matmul_mx(
@@ -189,59 +190,61 @@ def tile_picked_modres_mlpgelu_p_kernel(tc, x_words, x_scales, gate, res, w1, w2
                 start=True,
                 stop=True,
             )
-            update = keep.tile([P, CHUNK], F32, name="update_first", align_bytes=64)
+            update = keep.tile([P, CHUNK], F32, name="update_first", align_bytes=ALIGN)
             nc.vector.tensor_tensor(update[:], y_bank[:], gate_first, MULT)
-            put(0, 0, CHUNK, update[:], old_upper[:, 0:CHUNK])
+            return update
 
-        def gated_rows(c, first):
+        def gated_product(c, first_row):
             codes, plane = h_mx[c]
-            y_bank = psum.tile([P, N - first], F32, name="y_bank", tag=y_tags[c])
+            y_bank = psum.tile([P, N - first_row], F32, name="y_bank", tag=y_tags[c % 2])
             nc.tensor.matmul_mx(
                 out=y_bank[:],
                 lhsT=codes[:].bitcast(FP8X4),
                 lhsT_scale=plane[:],
-                rhs=w2_codes[:, first:N].bitcast(FP8X4),
-                rhs_scale=w2_plane[:, first:N],
+                rhs=w2_codes[:, first_row:N].bitcast(FP8X4),
+                rhs_scale=w2_plane[:, first_row:N],
                 start=True,
                 stop=True,
             )
-            gated = keep.tile([P, N - first], F32, name="gated_%d" % c)
+            gated = keep.tile([P, N - first_row], F32, name="gated_%d" % c)
             nc.scalar.activation(gated[:], y_bank[:], COPY, scale=gate_cols[:, c : c + 1])
             return gated
 
-        def turn_back(c, gated, count):
-            turned = psum.tile([P, count, CHUNK], F32, name="turned", tag=turn_tags[c])
-            for b in range(count):
+        def turn_back(c, gated, tag):
+            blocks = gated.shape[1] // P
+            turned = psum.tile([P, blocks, CHUNK], F32, name="turned", tag=tag)
+            for b in range(blocks):
                 nc.tensor.transpose(turned[:, b, :], gated[:, b * P : (b + 1) * P], identity[:])
-            update = keep.tile([P, count, CHUNK], F32, name="update_%d" % c, align_bytes=64)
+            update = keep.tile([P, blocks, CHUNK], F32, name="update_%d" % c, align_bytes=ALIGN)
             nc.scalar.copy(out=update[:], in_=turned[:])
             return update
 
-        old_lower_first = keep.tile([P, 2 * CHUNK], F32, name="old_lower_first", align_bytes=64)
-        nc.vector.tensor_copy(old_lower_first[:], stream[1][:].indirect(entries(0, 2 * CHUNK)))
+        old_lower_first = keep.tile([P, HALF_LIST], F32, name="old_lower_first", align_bytes=ALIGN)
+        nc.vector.tensor_copy(old_lower_first[:], stream[LOWER][:].indirect(entries(0, HALF_LIST)))
         hidden(0)
-        old_lower_rest = keep.tile([P, 2 * CHUNK], F32, name="old_lower_rest", tag="h_0", align_bytes=64)
-        nc.vector.tensor_copy(old_lower_rest[:], stream[1][:].indirect(entries(2 * CHUNK, S)))
+        old_lower_rest = keep.tile([P, HALF_LIST], F32, name="old_lower_rest", tag="h_0", align_bytes=ALIGN)
+        nc.vector.tensor_copy(old_lower_rest[:], stream[LOWER][:].indirect(entries(HALF_LIST, S)))
         hidden(1)
-        second_direct()
-        update = turn_back(0, gated_rows(0, P), 1)
+        put(UPPER, 0, CHUNK, first_upper_update()[:], old_upper[:, 0:CHUNK])
+        lower_0 = turn_back(0, gated_product(0, P), "h_a")
         hidden(2)
         hidden(3)
-        put(1, 0, CHUNK, update[:, 0, :], old_lower_first[:, 0:CHUNK])
-        update = turn_back(1, gated_rows(1, 0), 2)
-        put(0, CHUNK, 2 * CHUNK, update[:, 0, :], old_upper[:, CHUNK : 2 * CHUNK])
-        put(1, CHUNK, 2 * CHUNK, update[:, 1, :], old_lower_first[:, CHUNK : 2 * CHUNK])
-        turned_upper = psum.tile([P, 2 * CHUNK], F32, name="turned_upper", tag="h_a")
-        for c in range(2, CHUNKS):
-            gated = gated_rows(c, 0)
-            cols = slice((c - 2) * CHUNK, (c - 1) * CHUNK)
-            nc.tensor.transpose(turned_upper[:, cols], gated[:, 0:P], identity[:])
-            nc.tensor.transpose(turned_last[:, cols], gated[:, P:N], identity[:])
-        update_upper = keep.tile([P, 2 * CHUNK], F32, name="update_upper", align_bytes=64)
-        nc.scalar.copy(out=update_upper[:], in_=turned_upper[:])
-        put(0, 2 * CHUNK, S, update_upper[:], old_upper[:, 2 * CHUNK : S])
-        nc.sync.dma_start(out=out[0:P, :], in_=stream[0][:])
-        update_last = keep.tile([P, 2 * CHUNK], F32, name="update_last", align_bytes=64)
-        nc.scalar.copy(out=update_last[:], in_=turned_last[:])
-        put(1, 2 * CHUNK, S, update_last[:], old_lower_rest[:])
-        nc.sync.dma_start(out=out[P : 2 * P, :], in_=stream[1][:])
+        put(LOWER, 0, CHUNK, lower_0[:, 0, :], old_lower_first[:, 0:CHUNK])
+        both_1 = turn_back(1, gated_product(1, 0), "turn")
+        put(UPPER, CHUNK, HALF_LIST, both_1[:, UPPER, :], old_upper[:, CHUNK:HALF_LIST])
+        put(LOWER, CHUNK, HALF_LIST, both_1[:, LOWER, :], old_lower_first[:, CHUNK:HALF_LIST])
+
+        turned_upper = psum.tile([P, HALF_LIST], F32, name="turned_upper", tag="h_a")
+        for c in range(CHUNKS // 2, CHUNKS):
+            gated = gated_product(c, 0)
+            place = slice(c * CHUNK - HALF_LIST, (c + 1) * CHUNK - HALF_LIST)
+            nc.tensor.transpose(turned_upper[:, place], gated[:, 0:P], identity[:])
+            nc.tensor.transpose(turned_lower[:, place], gated[:, P:N], identity[:])
+        upper_rest = keep.tile([P, HALF_LIST], F32, name="upper_rest", align_bytes=ALIGN)
+        nc.scalar.copy(out=upper_rest[:], in_=turned_upper[:])
+        put(UPPER, HALF_LIST, S, upper_rest[:], old_upper[:, HALF_LIST:S])
+        nc.sync.dma_start(out=out[0:P, :], in_=stream[UPPER][:])
+        lower_rest = keep.tile([P, HALF_LIST], F32, name="lower_rest", align_bytes=ALIGN)
+        nc.scalar.copy(out=lower_rest[:], in_=turned_lower[:])
+        put(LOWER, HALF_LIST, S, lower_rest[:], old_lower_rest[:])
+        nc.sync.dma_start(out=out[P:N, :], in_=stream[LOWER][:])

@@ -48,9 +48,12 @@ def tile_picked_modres_mlpgelu_p_kernel(
 
         x_scale_window = keep.tile([P, T], U8, name="x_scale_window", align_bytes=ALIGN)
         identity = keep.tile([P, P], F32, name="identity")
-        nc.vector.memset(x_scale_window[:].bitcast(I32), 0)
+        nc.gpsimd.memset(x_scale_window[:].bitcast(I32), 0)
         w2_plane = keep.tile([P, N], U8, name="w2_plane", align_bytes=ALIGN)
         nc.gpsimd.memset(w2_plane[:].bitcast(I32), 0)
+        gate_rows = keep.tile([P, CHUNK], F32, name="gate_rows", align_bytes=ALIGN)
+        nc.gpsimd.memset(gate_rows[:], 0.0)
+        nc.scalar.dma_start(out=gate_rows[0:CHUNKS, :], in_=gate[0].rearrange("(c j) -> c j", j=CHUNK))
         make_identity(nc, identity[:])
 
         def load_w1(name, z, first, last):
@@ -67,8 +70,8 @@ def tile_picked_modres_mlpgelu_p_kernel(
             )
             return window
 
-        nc.sync.dma_start(offsets[:], offs)
         x_window = [load_x(0)]
+        nc.sync.dma_start(offsets[:], offs)
         for q in range(QUADRANTS):
             nc.sync.dma_start(
                 out=x_scale_window[QUADRANT * q : QUADRANT * q + SCALE_ROWS * PASSES, :].bitcast(I32),
@@ -91,6 +94,8 @@ def tile_picked_modres_mlpgelu_p_kernel(
             out=w2_codes[:].bitcast(I32),
             in_=w2_words[0].rearrange("p n r -> p (n r)").bitcast(I32),
         )
+        gate_first = keep.tile([P, CHUNK], F32, name="gate_first", align_bytes=ALIGN)
+        nc.sync.dma_start(out=gate_first[:], in_=gate[:, 0:CHUNK])
 
         x_plane = keep.tile([P, S], U8, name="x_plane", align_bytes=ALIGN)
         nc.vector.tensor_copy(x_plane[:], x_scale_window[:].indirect(offsets[:]))
@@ -117,12 +122,25 @@ def tile_picked_modres_mlpgelu_p_kernel(
 
         round_w1(nc.vector.tensor_copy, w1_first, 0, 0, 0)
         round_w1(nc.scalar.copy, w1_first, 0, 0, 1)
-        quantize_w1(0, 0, PACK)
-        for pair in range(2):
-            round_w1(nc.scalar.copy, w1_left, 1, 0, pair)
+        quantize_w1(0, 0, 2)
+        round_w1(nc.vector.tensor_copy, w1_left, 1, 0, 0)
+        round_w1(nc.scalar.copy, w1_left, 1, 0, 1)
+        quantize_w1(0, 2, PACK)
 
         x_codes = [keep.tile([P, S], U32, name="x_codes_%d" % z, align_bytes=ALIGN) for z in range(PASSES)]
         nc.vector.tensor_copy(x_codes[0][:], x_window[0][:].indirect(offsets[:]))
+
+        warm_bank = psum.tile([P, S], F32, name="warm_bank", tag="y_b")
+        for repeat in range(2):
+            nc.tensor.matmul_mx(
+                out=warm_bank[:],
+                lhsT=w1_codes[0][:, 2 * P : 3 * P].bitcast(FP8X4),
+                lhsT_scale=w1_plane[0][:, 2 * P : 3 * P],
+                rhs=x_codes[0][:].bitcast(FP8X4),
+                rhs_scale=x_plane[:],
+                start=True,
+                stop=True,
+            )
 
         round_w1(nc.vector.tensor_copy, w1_right, 1, HALF_H // PACK, 0)
         round_w1(nc.scalar.copy, w1_right, 1, HALF_H // PACK, 1)
@@ -132,23 +150,16 @@ def tile_picked_modres_mlpgelu_p_kernel(
         nc.vector.tensor_copy(x_codes[1][:, 0:CHUNK], x_window[1][:].indirect(entries(0, CHUNK)))
         nc.vector.tensor_copy(x_codes[1][:, CHUNK:S], x_window[1][:].indirect(entries(CHUNK, S)))
 
-        gates = keep.tile([P, 2 * CHUNK], F32, name="gates", tag="w1_right", align_bytes=ALIGN)
-        gate_first = gates[:, 0:CHUNK]
-        gate_rows = gates[:, CHUNK : 2 * CHUNK]
-        nc.gpsimd.memset(gate_rows, 0.0)
-        nc.scalar.dma_start(out=gate_first, in_=gate[:, 0:CHUNK])
-        nc.scalar.dma_start(out=gates[0:CHUNKS, CHUNK : 2 * CHUNK], in_=gate[0].rearrange("(c j) -> c j", j=CHUNK))
         gate_bank = psum.tile([P, P], F32, name="gate_bank", tag="turn")
-        nc.tensor.transpose(gate_bank[:], gate_rows, identity[:])
+        nc.tensor.transpose(gate_bank[:], gate_rows[:], identity[:])
         gate_cols = keep.tile([P, CHUNKS], F32, name="gate_cols")
         nc.scalar.copy(out=gate_cols[:], in_=gate_bank[:, 0:CHUNKS])
 
         old_upper = keep.tile([P, S], F32, name="old_upper", align_bytes=ALIGN)
         nc.vector.tensor_copy(old_upper[:], stream[UPPER][:].indirect(offsets[:]))
 
-        turned_lower = psum.tile([P, HALF_LIST], F32, name="turned_lower")
-        h_tags = ["h_a", "h_b", "h_c", "h_b"]
-        y_tags = ["y_even", "y_odd"]
+        h_tags = ["h_a", "h_b", "h_c", "h_d"]
+        y_tags = ["y_a", "y_b", "y_c", "y_a"]
         h_mx = {}
 
         def hidden(c):
@@ -180,33 +191,33 @@ def tile_picked_modres_mlpgelu_p_kernel(
 
         def first_upper_update():
             codes, plane = h_mx[0]
-            y_bank = psum.tile([P, CHUNK], F32, name="y_first")
+            y_bank = psum.tile([P, CHUNK], F32, name="y_first", tag="y_c")
             nc.tensor.matmul_mx(
                 out=y_bank[:],
-                lhsT=w2_codes[:, 0:P].bitcast(FP8X4),
-                lhsT_scale=w2_plane[:, 0:P],
+                lhsT=w2_codes[:, P:N].bitcast(FP8X4),
+                lhsT_scale=w2_plane[:, P:N],
                 rhs=codes[:].bitcast(FP8X4),
                 rhs_scale=plane[:],
                 start=True,
                 stop=True,
             )
             update = keep.tile([P, CHUNK], F32, name="update_first", align_bytes=ALIGN)
-            nc.vector.tensor_tensor(update[:], y_bank[:], gate_first, MULT)
+            nc.vector.tensor_tensor(update[:], y_bank[:], gate_first[:], MULT)
             return update
 
-        def gated_product(c, first_row):
+        def gated_product(c, rows):
             codes, plane = h_mx[c]
-            y_bank = psum.tile([P, N - first_row], F32, name="y_bank", tag=y_tags[c % 2])
+            y_bank = psum.tile([P, rows], F32, name="y_bank", tag=y_tags[c])
             nc.tensor.matmul_mx(
                 out=y_bank[:],
                 lhsT=codes[:].bitcast(FP8X4),
                 lhsT_scale=plane[:],
-                rhs=w2_codes[:, first_row:N].bitcast(FP8X4),
-                rhs_scale=w2_plane[:, first_row:N],
+                rhs=w2_codes[:, 0:rows].bitcast(FP8X4),
+                rhs_scale=w2_plane[:, 0:rows],
                 start=True,
                 stop=True,
             )
-            gated = keep.tile([P, N - first_row], F32, name="gated_%d" % c)
+            gated = keep.tile([P, rows], F32, name="gated_%d" % c)
             nc.scalar.activation(gated[:], y_bank[:], COPY, scale=gate_cols[:, c : c + 1])
             return gated
 
@@ -220,31 +231,34 @@ def tile_picked_modres_mlpgelu_p_kernel(
             return update
 
         old_lower_first = keep.tile([P, HALF_LIST], F32, name="old_lower_first", align_bytes=ALIGN)
-        nc.vector.tensor_copy(old_lower_first[:], stream[LOWER][:].indirect(entries(0, HALF_LIST)))
+        old_lower_rest = keep.tile([P, HALF_LIST], F32, name="old_lower_rest", align_bytes=ALIGN)
         hidden(0)
-        old_lower_rest = keep.tile([P, HALF_LIST], F32, name="old_lower_rest", tag="h_0", align_bytes=ALIGN)
-        nc.vector.tensor_copy(old_lower_rest[:], stream[LOWER][:].indirect(entries(HALF_LIST, S)))
+        nc.vector.tensor_copy(old_lower_first[:], stream[LOWER][:].indirect(entries(0, HALF_LIST)))
         hidden(1)
-        put(UPPER, 0, CHUNK, first_upper_update()[:], old_upper[:, 0:CHUNK])
-        lower_0 = turn_back(0, gated_product(0, P), "h_a")
+        lower_0 = first_upper_update()
+        nc.vector.tensor_copy(old_lower_rest[:], stream[LOWER][:].indirect(entries(HALF_LIST, S)))
+        gated_0 = gated_product(0, P)
         hidden(2)
+        upper_0 = turn_back(0, gated_0, "h_a")
+        put(LOWER, 0, CHUNK, lower_0[:], old_lower_first[:, 0:CHUNK])
         hidden(3)
-        put(LOWER, 0, CHUNK, lower_0[:, 0, :], old_lower_first[:, 0:CHUNK])
-        both_1 = turn_back(1, gated_product(1, 0), "turn")
-        put(UPPER, CHUNK, HALF_LIST, both_1[:, UPPER, :], old_upper[:, CHUNK:HALF_LIST])
+        put(UPPER, 0, CHUNK, upper_0[:, 0, :], old_upper[:, 0:CHUNK])
+        both_1 = turn_back(1, gated_product(1, N), "h_b")
         put(LOWER, CHUNK, HALF_LIST, both_1[:, LOWER, :], old_lower_first[:, CHUNK:HALF_LIST])
+        put(UPPER, CHUNK, HALF_LIST, both_1[:, UPPER, :], old_upper[:, CHUNK:HALF_LIST])
 
-        turned_upper = psum.tile([P, HALF_LIST], F32, name="turned_upper", tag="h_a")
+        turned_lower = psum.tile([P, HALF_LIST], F32, name="turned_lower", tag="h_c")
+        turned_upper = psum.tile([P, HALF_LIST], F32, name="turned_upper", tag="turn")
         for c in range(CHUNKS // 2, CHUNKS):
-            gated = gated_product(c, 0)
+            gated = gated_product(c, N)
             place = slice(c * CHUNK - HALF_LIST, (c + 1) * CHUNK - HALF_LIST)
-            nc.tensor.transpose(turned_upper[:, place], gated[:, 0:P], identity[:])
             nc.tensor.transpose(turned_lower[:, place], gated[:, P:N], identity[:])
-        upper_rest = keep.tile([P, HALF_LIST], F32, name="upper_rest", align_bytes=ALIGN)
-        nc.scalar.copy(out=upper_rest[:], in_=turned_upper[:])
-        put(UPPER, HALF_LIST, S, upper_rest[:], old_upper[:, HALF_LIST:S])
-        nc.sync.dma_start(out=out[0:P, :], in_=stream[UPPER][:])
+            nc.tensor.transpose(turned_upper[:, place], gated[:, 0:P], identity[:])
         lower_rest = keep.tile([P, HALF_LIST], F32, name="lower_rest", align_bytes=ALIGN)
         nc.scalar.copy(out=lower_rest[:], in_=turned_lower[:])
         put(LOWER, HALF_LIST, S, lower_rest[:], old_lower_rest[:])
         nc.sync.dma_start(out=out[P:N, :], in_=stream[LOWER][:])
+        upper_rest = keep.tile([P, HALF_LIST], F32, name="upper_rest", align_bytes=ALIGN)
+        nc.scalar.copy(out=upper_rest[:], in_=turned_upper[:])
+        put(UPPER, HALF_LIST, S, upper_rest[:], old_upper[:, HALF_LIST:S])
+        nc.sync.dma_start(out=out[0:P, :], in_=stream[UPPER][:])

@@ -43,6 +43,10 @@ def tile_picked_modres_mlpgelu_p_kernel(
 
         offsets = keep.tile([P, S // LIST_ROWS], U16, name="offsets")
 
+        table_warm = keep.tile([P, 2], F32, name="table_warm")
+        nc.vector.memset(table_warm[:, 0:1], 0.0)
+        nc.scalar.activation(table_warm[:, 1:2], table_warm[:, 0:1], GELU)
+
         def entries(first, last):
             return offsets[:, first // LIST_ROWS : last // LIST_ROWS]
 
@@ -94,8 +98,6 @@ def tile_picked_modres_mlpgelu_p_kernel(
             out=w2_codes[:].bitcast(I32),
             in_=w2_words[0].rearrange("p n r -> p (n r)").bitcast(I32),
         )
-        gate_first = keep.tile([P, CHUNK], F32, name="gate_first", align_bytes=ALIGN)
-        nc.sync.dma_start(out=gate_first[:], in_=gate[:, 0:CHUNK])
 
         x_plane = keep.tile([P, S], U8, name="x_plane", align_bytes=ALIGN)
         nc.vector.tensor_copy(x_plane[:], x_scale_window[:].indirect(offsets[:]))
@@ -144,11 +146,14 @@ def tile_picked_modres_mlpgelu_p_kernel(
 
         round_w1(nc.vector.tensor_copy, w1_right, 1, HALF_H // PACK, 0)
         round_w1(nc.scalar.copy, w1_right, 1, HALF_H // PACK, 1)
+        gate_first = keep.tile([P, CHUNK], F32, name="gate_first", tag="w1_right", align_bytes=ALIGN)
+        nc.scalar.dma_start(out=gate_first[:], in_=gate[:, 0:CHUNK])
         quantize_w1(1, 0, 2)
         quantize_w1(1, 2, PACK)
 
         nc.vector.tensor_copy(x_codes[1][:, 0:CHUNK], x_window[1][:].indirect(entries(0, CHUNK)))
-        nc.vector.tensor_copy(x_codes[1][:, CHUNK:S], x_window[1][:].indirect(entries(CHUNK, S)))
+        nc.vector.tensor_copy(x_codes[1][:, CHUNK:HALF_LIST], x_window[1][:].indirect(entries(CHUNK, HALF_LIST)))
+        nc.vector.tensor_copy(x_codes[1][:, HALF_LIST:S], x_window[1][:].indirect(entries(HALF_LIST, S)))
 
         gate_bank = psum.tile([P, P], F32, name="gate_bank", tag="turn")
         nc.tensor.transpose(gate_bank[:], gate_rows[:], identity[:])
@@ -179,7 +184,7 @@ def tile_picked_modres_mlpgelu_p_kernel(
                     )
             h = keep.tile([P, CHUNK, PACK], BF16, name="h", tag="h_%d" % c, align_bytes=ALIGN)
             nc.scalar.activation(h[:], bank[:].rearrange("p t n -> p n t"), GELU)
-            codes = keep.tile([P, CHUNK], U32, name="h_codes_%d" % c, align_bytes=ALIGN)
+            codes = keep.tile([P, CHUNK], U32, name="h_codes", tag="h_codes_%d" % c, align_bytes=ALIGN)
             plane = keep.tile([P, CHUNK], U8, name="h_plane_%d" % c, align_bytes=ALIGN)
             nc.vector.quantize_mx(
                 out=codes[:].bitcast(FP8X4), scales=plane[:], in_=h[:].rearrange("p n t -> p (n t)")
@@ -231,13 +236,13 @@ def tile_picked_modres_mlpgelu_p_kernel(
             return update
 
         old_lower_first = keep.tile([P, HALF_LIST], F32, name="old_lower_first", align_bytes=ALIGN)
-        old_lower_rest = keep.tile([P, HALF_LIST], F32, name="old_lower_rest", align_bytes=ALIGN)
         hidden(0)
         nc.vector.tensor_copy(old_lower_first[:], stream[LOWER][:].indirect(entries(0, HALF_LIST)))
         hidden(1)
         lower_0 = first_upper_update()
-        nc.vector.tensor_copy(old_lower_rest[:], stream[LOWER][:].indirect(entries(HALF_LIST, S)))
         gated_0 = gated_product(0, P)
+        old_lower_rest = keep.tile([P, HALF_LIST], F32, name="old_lower_rest", tag="h_codes_0", align_bytes=ALIGN)
+        nc.vector.tensor_copy(old_lower_rest[:], stream[LOWER][:].indirect(entries(HALF_LIST, S)))
         hidden(2)
         upper_0 = turn_back(0, gated_0, "h_a")
         put(LOWER, 0, CHUNK, lower_0[:], old_lower_first[:, 0:CHUNK])

@@ -30,6 +30,7 @@ CHUNKS = S // CHUNK
 HALF_LIST = S // 2
 HALF_H = H // 2
 UPPER, LOWER = 0, 1
+WARM_PASSES = 2
 ALIGN = 64
 
 
@@ -133,7 +134,7 @@ def tile_picked_modres_mlpgelu_p_kernel(
         nc.vector.tensor_copy(x_codes[0][:], x_window[0][:].indirect(offsets[:]))
 
         warm_bank = psum.tile([P, S], F32, name="warm_bank", tag="y_b")
-        for repeat in range(2):
+        for repeat in range(WARM_PASSES):
             nc.tensor.matmul_mx(
                 out=warm_bank[:],
                 lhsT=w1_codes[0][:, 2 * P : 3 * P].bitcast(FP8X4),
@@ -167,7 +168,7 @@ def tile_picked_modres_mlpgelu_p_kernel(
         y_tags = ["y_a", "y_b", "y_c", "y_a"]
         h_mx = {}
 
-        def hidden(c):
+        def gelu_of(c, h):
             cols = slice(c * CHUNK, (c + 1) * CHUNK)
             bank = psum.tile([P, PACK, CHUNK], F32, name="h_bank", tag=h_tags[c])
             for t in range(PACK):
@@ -182,27 +183,36 @@ def tile_picked_modres_mlpgelu_p_kernel(
                         start=(z == 0),
                         stop=(z == PASSES - 1),
                     )
-            h = keep.tile([P, CHUNK, PACK], BF16, name="h", tag="h_%d" % c, align_bytes=ALIGN)
-            nc.scalar.activation(h[:], bank[:].rearrange("p t n -> p n t"), GELU)
-            codes = keep.tile([P, CHUNK], U32, name="h_codes", tag="h_codes_%d" % c, align_bytes=ALIGN)
-            plane = keep.tile([P, CHUNK], U8, name="h_plane_%d" % c, align_bytes=ALIGN)
+            nc.scalar.activation(h, bank[:].rearrange("p t n -> p n t"), GELU)
+
+        def quantize_h(first, h):
+            width = h.shape[1]
+            codes = keep.tile([P, width], U32, name="h_codes", tag="h_codes_%d" % first, align_bytes=ALIGN)
+            plane = keep.tile([P, width], U8, name="h_plane_%d" % first, align_bytes=ALIGN)
             nc.vector.quantize_mx(
                 out=codes[:].bitcast(FP8X4), scales=plane[:], in_=h[:].rearrange("p n t -> p (n t)")
             )
-            h_mx[c] = (codes, plane)
+            for c in range(width // CHUNK):
+                cols = slice(c * CHUNK, (c + 1) * CHUNK)
+                h_mx[first + c] = (codes[:, cols], plane[:, cols])
+
+        def hidden(c):
+            h = keep.tile([P, CHUNK, PACK], BF16, name="h_%d" % c, align_bytes=ALIGN)
+            gelu_of(c, h[:])
+            quantize_h(c, h)
 
         def put(b, first, last, update, old):
             nc.vector.tensor_tensor(stream[b][:].indirect(entries(first, last)), update, old, ADD)
 
-        def first_upper_update():
+        def first_lower_update():
             codes, plane = h_mx[0]
             y_bank = psum.tile([P, CHUNK], F32, name="y_first", tag="y_c")
             nc.tensor.matmul_mx(
                 out=y_bank[:],
                 lhsT=w2_codes[:, P:N].bitcast(FP8X4),
                 lhsT_scale=w2_plane[:, P:N],
-                rhs=codes[:].bitcast(FP8X4),
-                rhs_scale=plane[:],
+                rhs=codes.bitcast(FP8X4),
+                rhs_scale=plane,
                 start=True,
                 stop=True,
             )
@@ -215,8 +225,8 @@ def tile_picked_modres_mlpgelu_p_kernel(
             y_bank = psum.tile([P, rows], F32, name="y_bank", tag=y_tags[c])
             nc.tensor.matmul_mx(
                 out=y_bank[:],
-                lhsT=codes[:].bitcast(FP8X4),
-                lhsT_scale=plane[:],
+                lhsT=codes.bitcast(FP8X4),
+                lhsT_scale=plane,
                 rhs=w2_codes[:, 0:rows].bitcast(FP8X4),
                 rhs_scale=w2_plane[:, 0:rows],
                 start=True,
@@ -239,14 +249,16 @@ def tile_picked_modres_mlpgelu_p_kernel(
         hidden(0)
         nc.vector.tensor_copy(old_lower_first[:], stream[LOWER][:].indirect(entries(0, HALF_LIST)))
         hidden(1)
-        lower_0 = first_upper_update()
+        lower_0 = first_lower_update()
         gated_0 = gated_product(0, P)
         old_lower_rest = keep.tile([P, HALF_LIST], F32, name="old_lower_rest", tag="h_codes_0", align_bytes=ALIGN)
         nc.vector.tensor_copy(old_lower_rest[:], stream[LOWER][:].indirect(entries(HALF_LIST, S)))
-        hidden(2)
+        h_rest = keep.tile([P, HALF_LIST, PACK], BF16, name="h_rest", align_bytes=ALIGN)
+        gelu_of(2, h_rest[:, 0:CHUNK, :])
         upper_0 = turn_back(0, gated_0, "h_a")
         put(LOWER, 0, CHUNK, lower_0[:], old_lower_first[:, 0:CHUNK])
-        hidden(3)
+        gelu_of(3, h_rest[:, CHUNK:HALF_LIST, :])
+        quantize_h(2, h_rest)
         put(UPPER, 0, CHUNK, upper_0[:, 0, :], old_upper[:, 0:CHUNK])
         both_1 = turn_back(1, gated_product(1, N), "h_b")
         put(LOWER, CHUNK, HALF_LIST, both_1[:, LOWER, :], old_lower_first[:, CHUNK:HALF_LIST])

@@ -30,7 +30,8 @@ CHUNKS = S // CHUNK
 HALF_LIST = S // 2
 HALF_H = H // 2
 UPPER, LOWER = 0, 1
-WARM_PASSES = 2
+WARM_WIDTHS = (S, S, HALF_LIST)
+OPENED = 2
 ALIGN = 64
 
 
@@ -83,13 +84,12 @@ def tile_picked_modres_mlpgelu_p_kernel(
                 in_=x_scales[:, SCALE_ROWS * q : SCALE_ROWS * (q + 1), :].bitcast(I32),
             )
         w1_first = load_w1("w1_first", 0, 0, H)
-        w1_left = load_w1("w1_left", 1, 0, HALF_H)
+        w1_second = load_w1("w1_second", 1, 0, H)
         for q in range(QUADRANTS):
             nc.sync.dma_start(
                 out=w2_plane[QUADRANT * q : QUADRANT * q + SCALE_ROWS, :].bitcast(I32),
                 in_=w2_scales[0, SCALE_ROWS * q : SCALE_ROWS * (q + 1), :].bitcast(I32),
             )
-        w1_right = load_w1("w1_right", 1, HALF_H, H)
         x_window.append(load_x(1))
         stream = [keep.tile([P, T], F32, name="stream_%d" % b, align_bytes=ALIGN) for b in (UPPER, LOWER)]
         for b in (UPPER, LOWER):
@@ -109,11 +109,11 @@ def tile_picked_modres_mlpgelu_p_kernel(
         w1_codes = [keep.tile([P, H], U32, name="w1_codes_%d" % z, align_bytes=ALIGN) for z in range(PASSES)]
         w1_plane = [keep.tile([P, H], U8, name="w1_plane_%d" % z, align_bytes=ALIGN) for z in range(PASSES)]
 
-        def round_w1(copy, raw, z, first_m, pair):
-            count = raw.shape[2] // PACK
+        def round_w1(copy, raw, z, first_m, pair, skip=0, count=None):
+            count = count or raw.shape[2] // PACK
             ts = slice(2 * pair, 2 * pair + 2)
-            dst = grouped[z][:, ts, first_m : first_m + count, :].rearrange("p t m j -> p m j t")
-            src = raw[:].rearrange("p j (m t) -> p m j t", t=PACK)[:, :, :, ts]
+            dst = grouped[z][:, ts, first_m + skip : first_m + skip + count, :].rearrange("p t m j -> p m j t")
+            src = raw[:].rearrange("p j (m t) -> p m j t", t=PACK)[:, skip : skip + count, :, ts]
             copy(out=dst, in_=src)
 
         def quantize_w1(z, first_t, last_t):
@@ -126,28 +126,46 @@ def tile_picked_modres_mlpgelu_p_kernel(
         round_w1(nc.vector.tensor_copy, w1_first, 0, 0, 0)
         round_w1(nc.scalar.copy, w1_first, 0, 0, 1)
         quantize_w1(0, 0, 2)
-        round_w1(nc.vector.tensor_copy, w1_left, 1, 0, 0)
-        round_w1(nc.scalar.copy, w1_left, 1, 0, 1)
         quantize_w1(0, 2, PACK)
 
         x_codes = [keep.tile([P, S], U32, name="x_codes_%d" % z, align_bytes=ALIGN) for z in range(PASSES)]
         nc.vector.tensor_copy(x_codes[0][:], x_window[0][:].indirect(offsets[:]))
 
         warm_bank = psum.tile([P, S], F32, name="warm_bank", tag="y_b")
-        for repeat in range(WARM_PASSES):
+        for width in WARM_WIDTHS:
             nc.tensor.matmul_mx(
-                out=warm_bank[:],
+                out=warm_bank[:, 0:width],
                 lhsT=w1_codes[0][:, 2 * P : 3 * P].bitcast(FP8X4),
                 lhsT_scale=w1_plane[0][:, 2 * P : 3 * P],
-                rhs=x_codes[0][:].bitcast(FP8X4),
-                rhs_scale=x_plane[:],
+                rhs=x_codes[0][:, 0:width].bitcast(FP8X4),
+                rhs_scale=x_plane[:, 0:width],
                 start=True,
                 stop=True,
             )
 
-        round_w1(nc.vector.tensor_copy, w1_right, 1, HALF_H // PACK, 0)
-        round_w1(nc.scalar.copy, w1_right, 1, HALF_H // PACK, 1)
-        gate_first = keep.tile([P, CHUNK], F32, name="gate_first", tag="w1_right", align_bytes=ALIGN)
+        h_tags = ["h_a", "h_b", "h_c", "h_d"]
+        h_banks = [psum.tile([P, PACK, CHUNK], F32, name="h_bank_%d" % c, tag=h_tags[c]) for c in range(CHUNKS)]
+
+        def first_product(c, t, z):
+            cols = slice(c * CHUNK, (c + 1) * CHUNK)
+            units = slice(t * P, (t + 1) * P)
+            nc.tensor.matmul_mx(
+                out=h_banks[c][:, t, :],
+                lhsT=w1_codes[z][:, units].bitcast(FP8X4),
+                lhsT_scale=w1_plane[z][:, units],
+                rhs=x_codes[z][:, cols].bitcast(FP8X4),
+                rhs_scale=x_plane[SCALE_ROWS * z : P, cols],
+                start=(z == 0),
+                stop=(z == PASSES - 1),
+            )
+
+        for c in range(CHUNKS):
+            first_product(c, OPENED, 0)
+
+        round_w1(nc.vector.tensor_copy, w1_second, 1, 0, 0)
+        round_w1(nc.vector.tensor_copy, w1_second, 1, 0, 1, 0, P // 4)
+        round_w1(nc.scalar.copy, w1_second, 1, 0, 1, P // 4, P - P // 4)
+        gate_first = keep.tile([P, CHUNK], F32, name="gate_first", tag="w1_second", align_bytes=ALIGN)
         nc.scalar.dma_start(out=gate_first[:], in_=gate[:, 0:CHUNK])
         quantize_w1(1, 0, 2)
         quantize_w1(1, 2, PACK)
@@ -164,25 +182,16 @@ def tile_picked_modres_mlpgelu_p_kernel(
         old_upper = keep.tile([P, S], F32, name="old_upper", align_bytes=ALIGN)
         nc.vector.tensor_copy(old_upper[:], stream[UPPER][:].indirect(offsets[:]))
 
-        h_tags = ["h_a", "h_b", "h_c", "h_d"]
         y_tags = ["y_a", "y_b", "y_c", "y_a"]
         h_mx = {}
 
         def gelu_of(c, h):
-            cols = slice(c * CHUNK, (c + 1) * CHUNK)
-            bank = psum.tile([P, PACK, CHUNK], F32, name="h_bank", tag=h_tags[c])
+            bank = h_banks[c]
+            first_product(c, OPENED, 1)
             for t in range(PACK):
-                units = slice(t * P, (t + 1) * P)
-                for z in range(PASSES):
-                    nc.tensor.matmul_mx(
-                        out=bank[:, t, :],
-                        lhsT=w1_codes[z][:, units].bitcast(FP8X4),
-                        lhsT_scale=w1_plane[z][:, units],
-                        rhs=x_codes[z][:, cols].bitcast(FP8X4),
-                        rhs_scale=x_plane[SCALE_ROWS * z : P, cols],
-                        start=(z == 0),
-                        stop=(z == PASSES - 1),
-                    )
+                if t != OPENED:
+                    for z in range(PASSES):
+                        first_product(c, t, z)
             nc.scalar.activation(h, bank[:].rearrange("p t n -> p n t"), GELU)
 
         def quantize_h(first, h):

@@ -84,21 +84,14 @@ def tile_picked_modres_mlpgelu_p_kernel(
                 in_=x_scales[:, SCALE_ROWS * q : SCALE_ROWS * (q + 1), :].bitcast(I32),
             )
         w1_first = load_w1("w1_first", 0, 0, H)
-        w1_second = load_w1("w1_second", 1, 0, H)
+        w1_left = load_w1("w1_left", 1, 0, HALF_H)
         for q in range(QUADRANTS):
             nc.sync.dma_start(
                 out=w2_plane[QUADRANT * q : QUADRANT * q + SCALE_ROWS, :].bitcast(I32),
                 in_=w2_scales[0, SCALE_ROWS * q : SCALE_ROWS * (q + 1), :].bitcast(I32),
             )
+        w1_right = load_w1("w1_right", 1, HALF_H, H)
         x_window.append(load_x(1))
-        stream = [keep.tile([P, T], F32, name="stream_%d" % b, align_bytes=ALIGN) for b in (UPPER, LOWER)]
-        for b in (UPPER, LOWER):
-            nc.sync.dma_start(out=stream[b][:], in_=res[b * P : (b + 1) * P, :])
-        w2_codes = keep.tile([P, N], U32, name="w2_codes", align_bytes=ALIGN)
-        nc.sync.dma_start(
-            out=w2_codes[:].bitcast(I32),
-            in_=w2_words[0].rearrange("p n r -> p (n r)").bitcast(I32),
-        )
 
         x_plane = keep.tile([P, S], U8, name="x_plane", align_bytes=ALIGN)
         nc.vector.tensor_copy(x_plane[:], x_scale_window[:].indirect(offsets[:]))
@@ -126,7 +119,23 @@ def tile_picked_modres_mlpgelu_p_kernel(
         round_w1(nc.vector.tensor_copy, w1_first, 0, 0, 0)
         round_w1(nc.scalar.copy, w1_first, 0, 0, 1)
         quantize_w1(0, 0, 2)
+        round_w1(nc.vector.tensor_copy, w1_left, 1, 0, 0)
+        round_w1(nc.scalar.copy, w1_left, 1, 0, 1)
         quantize_w1(0, 2, PACK)
+        stream = [
+            keep.tile([P, T], F32, name="stream_upper", tag="w1_first", align_bytes=ALIGN),
+            keep.tile([P, T], F32, name="stream_lower", align_bytes=ALIGN),
+        ]
+        nc.scalar.dma_start(out=stream[UPPER][:, 0 : T // 2], in_=res[0:P, 0 : T // 2])
+        nc.sync.dma_start(out=stream[UPPER][:, T // 2 : T], in_=res[0:P, T // 2 : T])
+        nc.sync.dma_start(out=stream[LOWER][:], in_=res[P:N, :])
+        gate_first = keep.tile([P, CHUNK], F32, name="gate_first", align_bytes=ALIGN)
+        nc.sync.dma_start(out=gate_first[:], in_=gate[:, 0:CHUNK])
+        w2_codes = keep.tile([P, N], U32, name="w2_codes", align_bytes=ALIGN)
+        nc.sync.dma_start(
+            out=w2_codes[:].bitcast(I32),
+            in_=w2_words[0].rearrange("p n r -> p (n r)").bitcast(I32),
+        )
 
         x_codes = [keep.tile([P, S], U32, name="x_codes_%d" % z, align_bytes=ALIGN) for z in range(PASSES)]
         nc.vector.tensor_copy(x_codes[0][:], x_window[0][:].indirect(offsets[:]))
@@ -162,11 +171,8 @@ def tile_picked_modres_mlpgelu_p_kernel(
         for c in range(CHUNKS):
             first_product(c, OPENED, 0)
 
-        round_w1(nc.vector.tensor_copy, w1_second, 1, 0, 0)
-        round_w1(nc.vector.tensor_copy, w1_second, 1, 0, 1, 0, P // 4)
-        round_w1(nc.scalar.copy, w1_second, 1, 0, 1, P // 4, P - P // 4)
-        gate_first = keep.tile([P, CHUNK], F32, name="gate_first", tag="w1_second", align_bytes=ALIGN)
-        nc.scalar.dma_start(out=gate_first[:], in_=gate[:, 0:CHUNK])
+        round_w1(nc.vector.tensor_copy, w1_right, 1, HALF_H // PACK, 0)
+        round_w1(nc.scalar.copy, w1_right, 1, HALF_H // PACK, 1)
         quantize_w1(1, 0, 2)
         quantize_w1(1, 2, PACK)
 

@@ -30,8 +30,6 @@ CHUNKS = S // CHUNK
 HALF_LIST = S // 2
 HALF_H = H // 2
 UPPER, LOWER = 0, 1
-WARM_WIDTHS = (S, S, HALF_LIST)
-OPENED = 2
 ALIGN = 64
 
 
@@ -140,18 +138,6 @@ def tile_picked_modres_mlpgelu_p_kernel(
         x_codes = [keep.tile([P, S], U32, name="x_codes_%d" % z, align_bytes=ALIGN) for z in range(PASSES)]
         nc.vector.tensor_copy(x_codes[0][:], x_window[0][:].indirect(offsets[:]))
 
-        warm_bank = psum.tile([P, S], F32, name="warm_bank", tag="y_b")
-        for width in WARM_WIDTHS:
-            nc.tensor.matmul_mx(
-                out=warm_bank[:, 0:width],
-                lhsT=w1_codes[0][:, 2 * P : 3 * P].bitcast(FP8X4),
-                lhsT_scale=w1_plane[0][:, 2 * P : 3 * P],
-                rhs=x_codes[0][:, 0:width].bitcast(FP8X4),
-                rhs_scale=x_plane[:, 0:width],
-                start=True,
-                stop=True,
-            )
-
         h_tags = ["h_a", "h_b", "h_c", "h_d"]
         h_banks = [psum.tile([P, PACK, CHUNK], F32, name="h_bank_%d" % c, tag=h_tags[c]) for c in range(CHUNKS)]
 
@@ -164,12 +150,13 @@ def tile_picked_modres_mlpgelu_p_kernel(
                 lhsT_scale=w1_plane[z][:, units],
                 rhs=x_codes[z][:, cols].bitcast(FP8X4),
                 rhs_scale=x_plane[SCALE_ROWS * z : P, cols],
-                start=(z == 0),
-                stop=(z == PASSES - 1),
+                start=(z == 0 and t == 0),
+                stop=(z == PASSES - 1 and t == PACK - 1),
             )
 
-        for c in range(CHUNKS):
-            first_product(c, OPENED, 0)
+        for t in range(PACK):
+            for c in range(CHUNKS):
+                first_product(c, t, 0)
 
         round_w1(nc.vector.tensor_copy, w1_right, 1, HALF_H // PACK, 0)
         round_w1(nc.scalar.copy, w1_right, 1, HALF_H // PACK, 1)
@@ -193,17 +180,14 @@ def tile_picked_modres_mlpgelu_p_kernel(
 
         def gelu_of(c, h):
             bank = h_banks[c]
-            first_product(c, OPENED, 1)
             for t in range(PACK):
-                if t != OPENED:
-                    for z in range(PASSES):
-                        first_product(c, t, z)
+                first_product(c, t, 1)
             nc.scalar.activation(h, bank[:].rearrange("p t n -> p n t"), GELU)
 
-        def quantize_h(first, h):
+        def quantize_h(first, h, codes_tag, plane_tag):
             width = h.shape[1]
-            codes = keep.tile([P, width], U32, name="h_codes", tag="h_codes_%d" % first, align_bytes=ALIGN)
-            plane = keep.tile([P, width], U8, name="h_plane_%d" % first, align_bytes=ALIGN)
+            codes = keep.tile([P, width], U32, name="h_codes", tag=codes_tag, align_bytes=ALIGN)
+            plane = keep.tile([P, width], U8, name="h_plane", tag=plane_tag, align_bytes=ALIGN)
             nc.vector.quantize_mx(
                 out=codes[:].bitcast(FP8X4), scales=plane[:], in_=h[:].rearrange("p n t -> p (n t)")
             )
@@ -214,7 +198,7 @@ def tile_picked_modres_mlpgelu_p_kernel(
         def hidden(c):
             h = keep.tile([P, CHUNK, PACK], BF16, name="h_%d" % c, align_bytes=ALIGN)
             gelu_of(c, h[:])
-            quantize_h(c, h)
+            quantize_h(c, h, "h_codes_%d" % c, "h_plane_%d" % c)
 
         def put(b, first, last, update, old):
             nc.vector.tensor_tensor(stream[b][:].indirect(entries(first, last)), update, old, ADD)
@@ -271,9 +255,9 @@ def tile_picked_modres_mlpgelu_p_kernel(
         h_rest = keep.tile([P, HALF_LIST, PACK], BF16, name="h_rest", align_bytes=ALIGN)
         gelu_of(2, h_rest[:, 0:CHUNK, :])
         upper_0 = turn_back(0, gated_0, "h_a")
-        put(LOWER, 0, CHUNK, lower_0[:], old_lower_first[:, 0:CHUNK])
         gelu_of(3, h_rest[:, CHUNK:HALF_LIST, :])
-        quantize_h(2, h_rest)
+        quantize_h(2, h_rest, "gate_first", "h_plane_rest")
+        put(LOWER, 0, CHUNK, lower_0[:], old_lower_first[:, 0:CHUNK])
         put(UPPER, 0, CHUNK, upper_0[:, 0, :], old_upper[:, 0:CHUNK])
         both_1 = turn_back(1, gated_product(1, N), "h_b")
         put(LOWER, CHUNK, HALF_LIST, both_1[:, LOWER, :], old_lower_first[:, CHUNK:HALF_LIST])

@@ -43,6 +43,9 @@ def tile_picked_modres_mlpgelu_p_kernel(
 
         offsets = keep.tile([P, S // LIST_ROWS], U16, name="offsets")
 
+        gate_cols = keep.tile([P, PACK], F32, name="gate_cols", tag="w1_grouped_0", align_bytes=ALIGN)
+        nc.scalar.dma_start(out=gate_cols[:], in_=gate[0].rearrange("(p r) -> p r", r=PACK))
+
         table_warm = keep.tile([P, 2], F32, name="table_warm")
         nc.vector.memset(table_warm[:, 0:1], 0.0)
         nc.scalar.activation(table_warm[:, 1:2], table_warm[:, 0:1], GELU)
@@ -51,19 +54,22 @@ def tile_picked_modres_mlpgelu_p_kernel(
             return offsets[:, first // LIST_ROWS : last // LIST_ROWS]
 
         x_scale_window = keep.tile([P, T], U8, name="x_scale_window", align_bytes=ALIGN)
-        identity = keep.tile([P, P], F32, name="identity")
         nc.gpsimd.memset(x_scale_window[:].bitcast(I32), 0)
         w2_plane = keep.tile([P, N], U8, name="w2_plane", align_bytes=ALIGN)
         nc.gpsimd.memset(w2_plane[:].bitcast(I32), 0)
-        gate_rows = keep.tile([P, CHUNK], F32, name="gate_rows", align_bytes=ALIGN)
-        nc.gpsimd.memset(gate_rows[:], 0.0)
-        nc.scalar.dma_start(out=gate_rows[0:CHUNKS, :], in_=gate[0].rearrange("(c j) -> c j", j=CHUNK))
+
+        identity = keep.tile([P, P], F32, name="identity")
         make_identity(nc, identity[:])
+        gate_spread = psum.tile([P, PACK, P], F32, name="gate_spread", tag="y_bank_1_1")
+        for r in range(PACK):
+            nc.tensor.transpose(gate_spread[:, r, :], gate_cols[:, r : r + 1].to_broadcast([P, P]), identity[:])
+        gate_all = keep.tile([P, S], F32, name="gate_all", align_bytes=ALIGN)
+        nc.scalar.copy(out=gate_all[:].rearrange("p (j r) -> p j r", r=PACK), in_=gate_spread[:].rearrange("p r j -> p j r"))
 
         def load_w1(name, z, first, last):
-            raw = keep.tile([P, PACK, last - first], F32, name=name, align_bytes=ALIGN)
-            rows = w1[z * K_PASS : (z + 1) * K_PASS, first:last]
-            nc.sync.dma_start(out=raw[:], in_=rows.rearrange("(p j) c -> p j c", j=PACK))
+            raw = keep.tile([P, last - first, H], F32, name=name, align_bytes=ALIGN)
+            rows = w1[z * K_PASS : (z + 1) * K_PASS, :]
+            nc.sync.dma_start(out=raw[:], in_=rows.rearrange("(p j) c -> p j c", j=PACK)[:, first:last, :])
             return raw
 
         def load_x(z):
@@ -81,14 +87,9 @@ def tile_picked_modres_mlpgelu_p_kernel(
                 out=x_scale_window[QUADRANT * q : QUADRANT * q + SCALE_ROWS * PASSES, :].bitcast(I32),
                 in_=x_scales[:, SCALE_ROWS * q : SCALE_ROWS * (q + 1), :].bitcast(I32),
             )
-        w1_first = load_w1("w1_first", 0, 0, H)
-        w1_left = load_w1("w1_left", 1, 0, HALF_H)
-        for q in range(QUADRANTS):
-            nc.sync.dma_start(
-                out=w2_plane[QUADRANT * q : QUADRANT * q + SCALE_ROWS, :].bitcast(I32),
-                in_=w2_scales[0, SCALE_ROWS * q : SCALE_ROWS * (q + 1), :].bitcast(I32),
-            )
-        w1_right = load_w1("w1_right", 1, HALF_H, H)
+        w1_first = load_w1("w1_first", 0, 0, PACK)
+        w1_left = load_w1("w1_left", 1, 0, 2)
+        w1_right = load_w1("w1_right", 1, 2, PACK)
         x_window.append(load_x(1))
 
         x_plane = keep.tile([P, S], U8, name="x_plane", align_bytes=ALIGN)
@@ -100,11 +101,10 @@ def tile_picked_modres_mlpgelu_p_kernel(
         w1_codes = [keep.tile([P, H], U32, name="w1_codes_%d" % z, align_bytes=ALIGN) for z in range(PASSES)]
         w1_plane = [keep.tile([P, H], U8, name="w1_plane_%d" % z, align_bytes=ALIGN) for z in range(PASSES)]
 
-        def round_w1(copy, raw, z, first_m, pair, skip=0, count=None):
-            count = count or raw.shape[2] // PACK
+        def round_w1(copy, raw, z, first_j, pair, ms=slice(0, P)):
             ts = slice(2 * pair, 2 * pair + 2)
-            dst = grouped[z][:, ts, first_m + skip : first_m + skip + count, :].rearrange("p t m j -> p m j t")
-            src = raw[:].rearrange("p j (m t) -> p m j t", t=PACK)[:, skip : skip + count, :, ts]
+            dst = grouped[z][:, ts, ms, first_j : first_j + raw.shape[1]].rearrange("p t m j -> p m j t")
+            src = raw[:].rearrange("p j (m t) -> p m j t", t=PACK)[:, ms, :, ts]
             copy(out=dst, in_=src)
 
         def quantize_w1(z, first_t, last_t):
@@ -120,22 +120,21 @@ def tile_picked_modres_mlpgelu_p_kernel(
         round_w1(nc.vector.tensor_copy, w1_left, 1, 0, 0)
         round_w1(nc.scalar.copy, w1_left, 1, 0, 1)
         quantize_w1(0, 2, PACK)
-        stream = [
-            keep.tile([P, T], F32, name="stream_upper", tag="w1_first", align_bytes=ALIGN),
-            keep.tile([P, T], F32, name="stream_lower", align_bytes=ALIGN),
-        ]
-        nc.scalar.dma_start(out=stream[UPPER][:, 0 : T // 2], in_=res[0:P, 0 : T // 2])
-        nc.sync.dma_start(out=stream[UPPER][:, T // 2 : T], in_=res[0:P, T // 2 : T])
+        stream = [keep.tile([P, T], F32, name="stream_%d" % b, align_bytes=ALIGN) for b in range(2)]
+        nc.sync.dma_start(out=stream[UPPER][:], in_=res[0:P, :])
         nc.sync.dma_start(out=stream[LOWER][:], in_=res[P:N, :])
-        gate_first = keep.tile([P, CHUNK], F32, name="gate_first", align_bytes=ALIGN)
-        nc.sync.dma_start(out=gate_first[:], in_=gate[:, 0:CHUNK])
         w2_codes = keep.tile([P, N], U32, name="w2_codes", align_bytes=ALIGN)
         nc.sync.dma_start(
             out=w2_codes[:].bitcast(I32),
             in_=w2_words[0].rearrange("p n r -> p (n r)").bitcast(I32),
         )
+        for q in range(QUADRANTS):
+            nc.sync.dma_start(
+                out=w2_plane[QUADRANT * q : QUADRANT * q + SCALE_ROWS, :].bitcast(I32),
+                in_=w2_scales[0, SCALE_ROWS * q : SCALE_ROWS * (q + 1), :].bitcast(I32),
+            )
 
-        x_codes = [keep.tile([P, S], U32, name="x_codes_%d" % z, align_bytes=ALIGN) for z in range(PASSES)]
+        x_codes = [keep.tile([P, S], U32, name="x_codes_0", align_bytes=ALIGN)]
         nc.vector.tensor_copy(x_codes[0][:], x_window[0][:].indirect(offsets[:]))
 
         h_tags = ["h_a", "h_b", "h_c", "h_d"]
@@ -148,7 +147,7 @@ def tile_picked_modres_mlpgelu_p_kernel(
                 out=h_banks[c][:, t, :],
                 lhsT=w1_codes[z][:, units].bitcast(FP8X4),
                 lhsT_scale=w1_plane[z][:, units],
-                rhs=x_codes[z][:, cols].bitcast(FP8X4),
+                rhs=(x_first[:] if (z, c) == (1, 0) else x_codes[z][:, cols]).bitcast(FP8X4),
                 rhs_scale=x_plane[SCALE_ROWS * z : P, cols],
                 start=(z == 0 and t == 0),
                 stop=(z == PASSES - 1 and t == PACK - 1),
@@ -158,123 +157,87 @@ def tile_picked_modres_mlpgelu_p_kernel(
             for c in range(CHUNKS):
                 first_product(c, t, 0)
 
-        round_w1(nc.vector.tensor_copy, w1_right, 1, HALF_H // PACK, 0)
-        round_w1(nc.scalar.copy, w1_right, 1, HALF_H // PACK, 1)
+        round_w1(nc.vector.tensor_copy, w1_right, 1, 2, 0)
+        round_w1(nc.scalar.copy, w1_right, 1, 2, 1)
         quantize_w1(1, 0, 2)
         quantize_w1(1, 2, PACK)
 
-        nc.vector.tensor_copy(x_codes[1][:, 0:CHUNK], x_window[1][:].indirect(entries(0, CHUNK)))
+        x_first = keep.tile([P, CHUNK], U32, name="x_first", align_bytes=ALIGN)
+        x_codes.append(keep.tile([P, S], U32, name="x_codes_1", tag="w1_right", align_bytes=ALIGN))
+        nc.vector.tensor_copy(x_first[:], x_window[1][:].indirect(entries(0, CHUNK)))
         nc.vector.tensor_copy(x_codes[1][:, CHUNK:HALF_LIST], x_window[1][:].indirect(entries(CHUNK, HALF_LIST)))
         nc.vector.tensor_copy(x_codes[1][:, HALF_LIST:S], x_window[1][:].indirect(entries(HALF_LIST, S)))
 
-        gate_bank = psum.tile([P, P], F32, name="gate_bank", tag="turn")
-        nc.tensor.transpose(gate_bank[:], gate_rows[:], identity[:])
-        gate_cols = keep.tile([P, CHUNKS], F32, name="gate_cols")
-        nc.scalar.copy(out=gate_cols[:], in_=gate_bank[:, 0:CHUNKS])
+        old = [keep.tile([P, S], F32, name="old_%d" % b, align_bytes=ALIGN) for b in range(2)]
 
-        old_upper = keep.tile([P, S], F32, name="old_upper", align_bytes=ALIGN)
-        nc.vector.tensor_copy(old_upper[:], stream[UPPER][:].indirect(offsets[:]))
+        def fetch_on_scalar(b, first, last):
+            nc.scalar.activation(old[b][:, first:last], stream[b][:].indirect(entries(first, last)), COPY)
 
-        y_tags = ["y_a", "y_b", "y_c", "y_a"]
-        h_mx = {}
+        def fetch_on_vector(b, first, last):
+            nc.vector.tensor_copy(old[b][:, first:last], stream[b][:].indirect(entries(first, last)))
 
-        def gelu_of(c, h):
-            bank = h_banks[c]
+        h_values = [keep.tile([P, CHUNK, PACK], BF16, name="h_%d" % c, align_bytes=ALIGN) for c in range(CHUNKS)]
+        h_codes = {}
+        h_plane = [keep.tile([P, CHUNK], U8, name="h_plane_%d" % c, align_bytes=ALIGN) for c in range(CHUNKS)]
+        y_banks = [
+            [psum.tile([P, HALF_LIST], F32, name="y_bank_%d_%d" % (b, half)) for half in range(2)] for b in range(2)
+        ]
+        gated = keep.tile([P, 2, S], F32, name="gated", align_bytes=ALIGN)
+        new_upper = keep.tile([P, S], F32, name="new_upper", align_bytes=ALIGN)
+
+        def gelu_of(c):
             for t in range(PACK):
                 first_product(c, t, 1)
-            nc.scalar.activation(h, bank[:].rearrange("p t n -> p n t"), GELU)
+            nc.scalar.activation(h_values[c][:], h_banks[c][:].rearrange("p t n -> p n t"), GELU)
 
-        def quantize_h(first, h, codes_tag, plane_tag):
-            width = h.shape[1]
-            codes = keep.tile([P, width], U32, name="h_codes", tag=codes_tag, align_bytes=ALIGN)
-            plane = keep.tile([P, width], U8, name="h_plane", tag=plane_tag, align_bytes=ALIGN)
+        def second_product(c, tag):
+            h_codes[c] = keep.tile([P, CHUNK], U32, name="h_codes", tag=tag, align_bytes=ALIGN)
             nc.vector.quantize_mx(
-                out=codes[:].bitcast(FP8X4), scales=plane[:], in_=h[:].rearrange("p n t -> p (n t)")
+                out=h_codes[c][:].bitcast(FP8X4), scales=h_plane[c][:], in_=h_values[c][:].rearrange("p n t -> p (n t)")
             )
-            for c in range(width // CHUNK):
-                cols = slice(c * CHUNK, (c + 1) * CHUNK)
-                h_mx[first + c] = (codes[:, cols], plane[:, cols])
+            for b in range(2):
+                rows = slice(b * P, (b + 1) * P)
+                nc.tensor.matmul_mx(
+                    out=y_banks[b][c // 2][:, (c % 2) * CHUNK : (c % 2 + 1) * CHUNK],
+                    lhsT=w2_codes[:, rows].bitcast(FP8X4),
+                    lhsT_scale=w2_plane[:, rows],
+                    rhs=h_codes[c][:].bitcast(FP8X4),
+                    rhs_scale=h_plane[c][:],
+                    start=True,
+                    stop=True,
+                )
 
-        def hidden(c):
-            h = keep.tile([P, CHUNK, PACK], BF16, name="h_%d" % c, align_bytes=ALIGN)
-            gelu_of(c, h[:])
-            quantize_h(c, h, "h_codes_%d" % c, "h_plane_%d" % c)
+        def gate_product(b, half, into):
+            cols = slice(half * HALF_LIST, (half + 1) * HALF_LIST)
+            nc.vector.tensor_tensor(into, y_banks[b][half][:], gate_all[:, cols], MULT)
 
-        def put(b, first, last, update, old):
-            nc.vector.tensor_tensor(stream[b][:].indirect(entries(first, last)), update, old, ADD)
+        def upper_sum(first, last, update):
+            nc.vector.tensor_tensor(new_upper[:, first:last], update, old[UPPER][:, first:last], ADD)
 
-        def first_lower_update():
-            codes, plane = h_mx[0]
-            y_bank = psum.tile([P, CHUNK], F32, name="y_first", tag="y_c")
-            nc.tensor.matmul_mx(
-                out=y_bank[:],
-                lhsT=w2_codes[:, P:N].bitcast(FP8X4),
-                lhsT_scale=w2_plane[:, P:N],
-                rhs=codes.bitcast(FP8X4),
-                rhs_scale=plane,
-                start=True,
-                stop=True,
+        def put_upper(first, last):
+            nc.scalar.activation(stream[UPPER][:].indirect(entries(first, last)), new_upper[:, first:last], COPY)
+
+        def put_lower(first, last):
+            nc.vector.tensor_tensor(
+                stream[LOWER][:].indirect(entries(first, last)), gated[:, LOWER, first:last], old[LOWER][:, first:last], ADD
             )
-            update = keep.tile([P, CHUNK], F32, name="update_first", align_bytes=ALIGN)
-            nc.vector.tensor_tensor(update[:], y_bank[:], gate_first[:], MULT)
-            return update
 
-        def gated_product(c, rows):
-            codes, plane = h_mx[c]
-            y_bank = psum.tile([P, rows], F32, name="y_bank", tag=y_tags[c])
-            nc.tensor.matmul_mx(
-                out=y_bank[:],
-                lhsT=codes.bitcast(FP8X4),
-                lhsT_scale=plane,
-                rhs=w2_codes[:, 0:rows].bitcast(FP8X4),
-                rhs_scale=w2_plane[:, 0:rows],
-                start=True,
-                stop=True,
-            )
-            gated = keep.tile([P, rows], F32, name="gated_%d" % c)
-            nc.scalar.activation(gated[:], y_bank[:], COPY, scale=gate_cols[:, c : c + 1])
-            return gated
-
-        def turn_back(c, gated, tag):
-            blocks = gated.shape[1] // P
-            turned = psum.tile([P, blocks, CHUNK], F32, name="turned", tag=tag)
-            for b in range(blocks):
-                nc.tensor.transpose(turned[:, b, :], gated[:, b * P : (b + 1) * P], identity[:])
-            update = keep.tile([P, blocks, CHUNK], F32, name="update_%d" % c, align_bytes=ALIGN)
-            nc.scalar.copy(out=update[:], in_=turned[:])
-            return update
-
-        old_lower_first = keep.tile([P, HALF_LIST], F32, name="old_lower_first", align_bytes=ALIGN)
-        hidden(0)
-        nc.vector.tensor_copy(old_lower_first[:], stream[LOWER][:].indirect(entries(0, HALF_LIST)))
-        hidden(1)
-        lower_0 = first_lower_update()
-        gated_0 = gated_product(0, P)
-        old_lower_rest = keep.tile([P, HALF_LIST], F32, name="old_lower_rest", tag="h_codes_0", align_bytes=ALIGN)
-        nc.vector.tensor_copy(old_lower_rest[:], stream[LOWER][:].indirect(entries(HALF_LIST, S)))
-        h_rest = keep.tile([P, HALF_LIST, PACK], BF16, name="h_rest", align_bytes=ALIGN)
-        gelu_of(2, h_rest[:, 0:CHUNK, :])
-        upper_0 = turn_back(0, gated_0, "h_a")
-        gelu_of(3, h_rest[:, CHUNK:HALF_LIST, :])
-        quantize_h(2, h_rest, "gate_first", "h_plane_rest")
-        put(LOWER, 0, CHUNK, lower_0[:], old_lower_first[:, 0:CHUNK])
-        put(UPPER, 0, CHUNK, upper_0[:, 0, :], old_upper[:, 0:CHUNK])
-        both_1 = turn_back(1, gated_product(1, N), "h_b")
-        put(LOWER, CHUNK, HALF_LIST, both_1[:, LOWER, :], old_lower_first[:, CHUNK:HALF_LIST])
-        put(UPPER, CHUNK, HALF_LIST, both_1[:, UPPER, :], old_upper[:, CHUNK:HALF_LIST])
-
-        turned_lower = psum.tile([P, HALF_LIST], F32, name="turned_lower", tag="h_c")
-        turned_upper = psum.tile([P, HALF_LIST], F32, name="turned_upper", tag="turn")
-        for c in range(CHUNKS // 2, CHUNKS):
-            gated = gated_product(c, N)
-            place = slice(c * CHUNK - HALF_LIST, (c + 1) * CHUNK - HALF_LIST)
-            nc.tensor.transpose(turned_lower[:, place], gated[:, P:N], identity[:])
-            nc.tensor.transpose(turned_upper[:, place], gated[:, 0:P], identity[:])
-        lower_rest = keep.tile([P, HALF_LIST], F32, name="lower_rest", align_bytes=ALIGN)
-        nc.scalar.copy(out=lower_rest[:], in_=turned_lower[:])
-        put(LOWER, HALF_LIST, S, lower_rest[:], old_lower_rest[:])
-        nc.sync.dma_start(out=out[P:N, :], in_=stream[LOWER][:])
-        upper_rest = keep.tile([P, HALF_LIST], F32, name="upper_rest", align_bytes=ALIGN)
-        nc.scalar.copy(out=upper_rest[:], in_=turned_upper[:])
-        put(UPPER, HALF_LIST, S, upper_rest[:], old_upper[:, HALF_LIST:S])
+        fetch_on_vector(UPPER, 0, S)
+        for c in range(CHUNKS - 1):
+            gelu_of(c)
+            second_product(c, "h_codes_%d" % c)
+        gelu_of(CHUNKS - 1)
+        fetch_on_scalar(LOWER, CHUNK, S)
+        fetch_on_vector(LOWER, 0, CHUNK)
+        gate_product(UPPER, 0, gated[:, LOWER, 0:HALF_LIST])
+        second_product(CHUNKS - 1, "h_codes_1")
+        upper_sum(0, HALF_LIST, gated[:, LOWER, 0:HALF_LIST])
+        gate_product(LOWER, 0, gated[:, LOWER, 0:HALF_LIST])
+        put_upper(0, HALF_LIST)
+        gate_product(UPPER, 1, gated[:, UPPER, HALF_LIST:S])
+        gate_product(LOWER, 1, gated[:, LOWER, HALF_LIST:S])
+        upper_sum(HALF_LIST, S, gated[:, UPPER, HALF_LIST:S])
+        put_upper(HALF_LIST, S)
         nc.sync.dma_start(out=out[0:P, :], in_=stream[UPPER][:])
+        put_lower(0, S)
+        nc.sync.dma_start(out=out[P:N, :], in_=stream[LOWER][:])

@@ -44,7 +44,6 @@ def tile_picked_modres_mlpgelu_p_kernel(
         offsets = keep.tile([P, S // LIST_ROWS], U16, name="offsets")
 
         gate_cols = keep.tile([P, PACK], F32, name="gate_cols", tag="w1_grouped_0", align_bytes=ALIGN)
-        nc.scalar.dma_start(out=gate_cols[:], in_=gate[0].rearrange("(p r) -> p r", r=PACK))
 
         table_warm = keep.tile([P, 2], F32, name="table_warm")
         nc.vector.memset(table_warm[:, 0:1], 0.0)
@@ -60,12 +59,6 @@ def tile_picked_modres_mlpgelu_p_kernel(
 
         identity = keep.tile([P, P], F32, name="identity")
         make_identity(nc, identity[:])
-        gate_spread = psum.tile([P, PACK, P], F32, name="gate_spread", tag="y_bank_1_1")
-        for r in range(PACK):
-            nc.tensor.transpose(gate_spread[:, r, :], gate_cols[:, r : r + 1].to_broadcast([P, P]), identity[:])
-        gate_all = keep.tile([P, S], F32, name="gate_all", align_bytes=ALIGN)
-        nc.scalar.copy(out=gate_all[:].rearrange("p (j r) -> p j r", r=PACK), in_=gate_spread[:].rearrange("p r j -> p j r"))
-
         def load_w1(name, z, first, last):
             raw = keep.tile([P, last - first, H], F32, name=name, align_bytes=ALIGN)
             rows = w1[z * K_PASS : (z + 1) * K_PASS, :]
@@ -82,11 +75,18 @@ def tile_picked_modres_mlpgelu_p_kernel(
 
         x_window = [load_x(0)]
         nc.sync.dma_start(offsets[:], offs)
+        nc.sync.dma_start(out=gate_cols[:], in_=gate[0].rearrange("(p r) -> p r", r=PACK))
         for q in range(QUADRANTS):
             nc.sync.dma_start(
                 out=x_scale_window[QUADRANT * q : QUADRANT * q + SCALE_ROWS * PASSES, :].bitcast(I32),
                 in_=x_scales[:, SCALE_ROWS * q : SCALE_ROWS * (q + 1), :].bitcast(I32),
             )
+        gate_spread = psum.tile([P, PACK, P], F32, name="gate_spread", tag="y_bank_1_1")
+        for r in range(PACK):
+            nc.tensor.transpose(gate_spread[:, r, :], gate_cols[:, r : r + 1].to_broadcast([P, P]), identity[:])
+        gate_all = keep.tile([P, S], F32, name="gate_all", align_bytes=ALIGN)
+        nc.scalar.copy(out=gate_all[:].rearrange("p (j r) -> p j r", r=PACK), in_=gate_spread[:].rearrange("p r j -> p j r"))
+
         w1_first = load_w1("w1_first", 0, 0, PACK)
         w1_left = load_w1("w1_left", 1, 0, 2)
         w1_right = load_w1("w1_right", 1, 2, PACK)
@@ -176,24 +176,25 @@ def tile_picked_modres_mlpgelu_p_kernel(
         def fetch_on_vector(b, first, last):
             nc.vector.tensor_copy(old[b][:, first:last], stream[b][:].indirect(entries(first, last)))
 
-        h_values = [keep.tile([P, CHUNK, PACK], BF16, name="h_%d" % c, align_bytes=ALIGN) for c in range(CHUNKS)]
+        gated = keep.tile([P, 2 * S], F32, name="gated", align_bytes=ALIGN)
+        h_values = [keep.tile([P, CHUNK * PACK], BF16, name="h_%d" % c, align_bytes=ALIGN)[:] for c in range(CHUNKS - 1)]
+        h_values.append(gated[:, S : S + HALF_LIST].bitcast(BF16))
         h_codes = {}
         h_plane = [keep.tile([P, CHUNK], U8, name="h_plane_%d" % c, align_bytes=ALIGN) for c in range(CHUNKS)]
         y_banks = [
             [psum.tile([P, HALF_LIST], F32, name="y_bank_%d_%d" % (b, half)) for half in range(2)] for b in range(2)
         ]
-        gated = keep.tile([P, 2, S], F32, name="gated", align_bytes=ALIGN)
         new_upper = keep.tile([P, S], F32, name="new_upper", align_bytes=ALIGN)
 
         def gelu_of(c):
             for t in range(PACK):
                 first_product(c, t, 1)
-            nc.scalar.activation(h_values[c][:], h_banks[c][:].rearrange("p t n -> p n t"), GELU)
+            nc.scalar.activation(h_values[c].rearrange("p (n t) -> p n t", t=PACK), h_banks[c][:].rearrange("p t n -> p n t"), GELU)
 
         def second_product(c, tag):
             h_codes[c] = keep.tile([P, CHUNK], U32, name="h_codes", tag=tag, align_bytes=ALIGN)
             nc.vector.quantize_mx(
-                out=h_codes[c][:].bitcast(FP8X4), scales=h_plane[c][:], in_=h_values[c][:].rearrange("p n t -> p (n t)")
+                out=h_codes[c][:].bitcast(FP8X4), scales=h_plane[c][:], in_=h_values[c]
             )
             for b in range(2):
                 rows = slice(b * P, (b + 1) * P)
@@ -219,7 +220,7 @@ def tile_picked_modres_mlpgelu_p_kernel(
 
         def put_lower(first, last):
             nc.vector.tensor_tensor(
-                stream[LOWER][:].indirect(entries(first, last)), gated[:, LOWER, first:last], old[LOWER][:, first:last], ADD
+                stream[LOWER][:].indirect(entries(first, last)), gated[:, S + first : S + last], old[LOWER][:, first:last], ADD
             )
 
         fetch_on_vector(UPPER, 0, S)
@@ -229,14 +230,14 @@ def tile_picked_modres_mlpgelu_p_kernel(
         gelu_of(CHUNKS - 1)
         fetch_on_scalar(LOWER, CHUNK, S)
         fetch_on_vector(LOWER, 0, CHUNK)
-        gate_product(UPPER, 0, gated[:, LOWER, 0:HALF_LIST])
+        gate_product(UPPER, 0, gated[:, 0:HALF_LIST])
         second_product(CHUNKS - 1, "h_codes_1")
-        upper_sum(0, HALF_LIST, gated[:, LOWER, 0:HALF_LIST])
-        gate_product(LOWER, 0, gated[:, LOWER, 0:HALF_LIST])
+        upper_sum(0, HALF_LIST, gated[:, 0:HALF_LIST])
+        gate_product(LOWER, 0, gated[:, S : S + HALF_LIST])
         put_upper(0, HALF_LIST)
-        gate_product(UPPER, 1, gated[:, UPPER, HALF_LIST:S])
-        gate_product(LOWER, 1, gated[:, LOWER, HALF_LIST:S])
-        upper_sum(HALF_LIST, S, gated[:, UPPER, HALF_LIST:S])
+        gate_product(UPPER, 1, gated[:, HALF_LIST:S])
+        gate_product(LOWER, 1, gated[:, S + HALF_LIST : 2 * S])
+        upper_sum(HALF_LIST, S, gated[:, HALF_LIST:S])
         put_upper(HALF_LIST, S)
         nc.sync.dma_start(out=out[0:P, :], in_=stream[UPPER][:])
         put_lower(0, S)

@@ -29,6 +29,7 @@ CHUNK = 128
 CHUNKS = S // CHUNK
 HALF_LIST = S // 2
 HALF_H = H // 2
+HEAD = 64
 UPPER, LOWER = 0, 1
 ALIGN = 64
 
@@ -228,13 +229,15 @@ def tile_picked_modres_mlpgelu_p_kernel(
             gelu_of(c)
             second_product(c, "h_codes_%d" % c)
         gelu_of(CHUNKS - 1)
-        fetch_on_scalar(LOWER, CHUNK, S)
-        fetch_on_vector(LOWER, 0, CHUNK)
+        fetch_on_scalar(LOWER, 0, S)
         gate_product(UPPER, 0, gated[:, 0:HALF_LIST])
         second_product(CHUNKS - 1, "h_codes_1")
-        upper_sum(0, HALF_LIST, gated[:, 0:HALF_LIST])
+        nc.vector.tensor_tensor(
+            stream[UPPER][:].indirect(entries(0, HEAD)), gated[:, 0:HEAD], old[UPPER][:, 0:HEAD], ADD
+        )
+        upper_sum(HEAD, HALF_LIST, gated[:, HEAD:HALF_LIST])
         gate_product(LOWER, 0, gated[:, S : S + HALF_LIST])
-        put_upper(0, HALF_LIST)
+        put_upper(HEAD, HALF_LIST)
         gate_product(UPPER, 1, gated[:, HALF_LIST:S])
         gate_product(LOWER, 1, gated[:, S + HALF_LIST : 2 * S])
         upper_sum(HALF_LIST, S, gated[:, HALF_LIST:S])

@@ -30,6 +30,7 @@ CHUNKS = S // CHUNK
 HALF_LIST = S // 2
 HALF_H = H // 2
 HEAD = 64
+SHORT = 64
 UPPER, LOWER = 0, 1
 ALIGN = 64
 
@@ -185,6 +186,7 @@ def tile_picked_modres_mlpgelu_p_kernel(
         y_banks = [
             [psum.tile([P, HALF_LIST], F32, name="y_bank_%d_%d" % (b, half)) for half in range(2)] for b in range(2)
         ]
+        y_first = psum.tile([P, CHUNK], F32, name="y_first", tag="h_a")
         new_upper = keep.tile([P, S], F32, name="new_upper", align_bytes=ALIGN)
 
         def gelu_of(c):
@@ -200,7 +202,7 @@ def tile_picked_modres_mlpgelu_p_kernel(
             for b in range(2):
                 rows = slice(b * P, (b + 1) * P)
                 nc.tensor.matmul_mx(
-                    out=y_banks[b][c // 2][:, (c % 2) * CHUNK : (c % 2 + 1) * CHUNK],
+                    out=y_first[:] if (b, c) == (UPPER, 0) else y_banks[b][c // 2][:, (c % 2) * CHUNK : (c % 2 + 1) * CHUNK],
                     lhsT=w2_codes[:, rows].bitcast(FP8X4),
                     lhsT_scale=w2_plane[:, rows],
                     rhs=h_codes[c][:].bitcast(FP8X4),
@@ -225,16 +227,21 @@ def tile_picked_modres_mlpgelu_p_kernel(
             )
 
         fetch_on_vector(UPPER, 0, S)
-        for c in range(CHUNKS - 1):
+        for c in range(CHUNKS):
             gelu_of(c)
-            second_product(c, "h_codes_%d" % c)
-        gelu_of(CHUNKS - 1)
-        fetch_on_scalar(LOWER, 0, S)
-        gate_product(UPPER, 0, gated[:, 0:HALF_LIST])
-        second_product(CHUNKS - 1, "h_codes_1")
+        fetch_on_scalar(LOWER, SHORT, S)
+        second_product(0, "h_codes_0")
+        second_product(1, "h_codes_1")
+        fetch_on_vector(LOWER, 0, SHORT)
+        nc.vector.tensor_tensor(gated[:, 0:CHUNK], y_first[:], gate_all[:, 0:CHUNK], MULT)
+        second_product(2, "h_codes_0")
+        nc.vector.tensor_tensor(
+            gated[:, CHUNK:HALF_LIST], y_banks[UPPER][0][:, CHUNK:HALF_LIST], gate_all[:, CHUNK:HALF_LIST], MULT
+        )
         nc.vector.tensor_tensor(
             stream[UPPER][:].indirect(entries(0, HEAD)), gated[:, 0:HEAD], old[UPPER][:, 0:HEAD], ADD
         )
+        second_product(CHUNKS - 1, "h_codes_1")
         upper_sum(HEAD, HALF_LIST, gated[:, HEAD:HALF_LIST])
         gate_product(LOWER, 0, gated[:, S : S + HALF_LIST])
         put_upper(HEAD, HALF_LIST)

@@ -183,10 +183,10 @@ def tile_picked_modres_mlpgelu_p_kernel(
         h_values.append(gated[:, S : S + HALF_LIST].bitcast(BF16))
         h_codes = {}
         h_plane = [keep.tile([P, CHUNK], U8, name="h_plane_%d" % c, align_bytes=ALIGN) for c in range(CHUNKS)]
+        y_first = psum.tile([P, CHUNK], F32, name="y_first", tag="y_bank_0_1")
         y_banks = [
             [psum.tile([P, HALF_LIST], F32, name="y_bank_%d_%d" % (b, half)) for half in range(2)] for b in range(2)
         ]
-        y_first = psum.tile([P, CHUNK], F32, name="y_first", tag="h_a")
         new_upper = keep.tile([P, S], F32, name="new_upper", align_bytes=ALIGN)
 
         def gelu_of(c):

@@ -32,7 +32,7 @@ HALF_H = H // 2
 HEAD = 64
 SHORT = 64
 UPPER, LOWER = 0, 1
-ALIGN = 64
+ALIGN = 256
 
 
 def tile_picked_modres_mlpgelu_p_kernel(
@@ -43,7 +43,7 @@ def tile_picked_modres_mlpgelu_p_kernel(
         keep = ctx.enter_context(tc.tile_pool(name="keep", bufs=1))
         psum = ctx.enter_context(tc.psum_pool(name="psum", bufs=1))
 
-        offsets = keep.tile([P, S // LIST_ROWS], U16, name="offsets")
+        offsets = keep.tile([P, S // LIST_ROWS], U16, name="offsets", align_bytes=ALIGN)
 
         gate_cols = keep.tile([P, PACK], F32, name="gate_cols", tag="w1_grouped_0", align_bytes=ALIGN)
 
@@ -59,7 +59,7 @@ def tile_picked_modres_mlpgelu_p_kernel(
         w2_plane = keep.tile([P, N], U8, name="w2_plane", align_bytes=ALIGN)
         nc.gpsimd.memset(w2_plane[:].bitcast(I32), 0)
 
-        identity = keep.tile([P, P], F32, name="identity")
+        identity = keep.tile([P, P], F32, name="identity", align_bytes=ALIGN)
         make_identity(nc, identity[:])
         def load_w1(name, z, first, last):
             raw = keep.tile([P, last - first, H], F32, name=name, align_bytes=ALIGN)

@@ -31,6 +31,7 @@ HALF_LIST = S // 2
 HALF_H = H // 2
 HEAD = 64
 SHORT = 64
+SCALAR_M = 96
 UPPER, LOWER = 0, 1
 ALIGN = 256
 
@@ -160,7 +161,8 @@ def tile_picked_modres_mlpgelu_p_kernel(
                 first_product(c, t, 0)
 
         round_w1(nc.vector.tensor_copy, w1_right, 1, 2, 0)
-        round_w1(nc.scalar.copy, w1_right, 1, 2, 1)
+        round_w1(nc.scalar.copy, w1_right, 1, 2, 1, slice(0, SCALAR_M))
+        round_w1(nc.vector.tensor_copy, w1_right, 1, 2, 1, slice(SCALAR_M, P))
         quantize_w1(1, 0, 2)
         quantize_w1(1, 2, PACK)
 

from contextlib import ExitStack

import concourse.mybir as mybir
from concourse.masks import make_identity

K, T, S, H, N = 1024, 1024, 512, 512, 256
FLOPS = 2 * S * H * (K + N)

F32 = mybir.dt.float32
BF16 = mybir.dt.bfloat16
I32 = mybir.dt.int32
U32 = mybir.dt.uint32
U16 = mybir.dt.uint16
U8 = mybir.dt.uint8
FP8X4 = mybir.dt.float8_e4m3fn_x4
GELU = mybir.ActivationFunctionType.Gelu_apprx_tanh
COPY = mybir.ActivationFunctionType.Copy
ADD = mybir.AluOpType.add
MULT = mybir.AluOpType.mult

P = 128
PACK = 4
K_PASS = P * PACK
PASSES = K // K_PASS
QUADRANTS, QUADRANT = 4, 32
SCALE_ROWS = 4
LIST_ROWS = 16
CHUNK = 128
CHUNKS = S // CHUNK
HALF_LIST = S // 2
HALF_H = H // 2
HEAD = 64
SHORT = 64
SCALAR_M = 96
UPPER, LOWER = 0, 1
ALIGN = 256


def tile_picked_modres_mlpgelu_p_kernel(
    tc, x_words, x_scales, gate, res, w1, w2_words, w2_scales, offs, out
):
    nc = tc.nc
    with ExitStack() as ctx:
        keep = ctx.enter_context(tc.tile_pool(name="keep", bufs=1))
        psum = ctx.enter_context(tc.psum_pool(name="psum", bufs=1))

        offsets = keep.tile([P, S // LIST_ROWS], U16, name="offsets", align_bytes=ALIGN)

        gate_cols = keep.tile([P, PACK], F32, name="gate_cols", tag="w1_grouped_0", align_bytes=ALIGN)

        table_warm = keep.tile([P, 2], F32, name="table_warm")
        nc.vector.memset(table_warm[:, 0:1], 0.0)
        nc.scalar.activation(table_warm[:, 1:2], table_warm[:, 0:1], GELU)

        def entries(first, last):
            return offsets[:, first // LIST_ROWS : last // LIST_ROWS]

        x_scale_window = keep.tile([P, T], U8, name="x_scale_window", align_bytes=ALIGN)
        nc.gpsimd.memset(x_scale_window[:].bitcast(I32), 0)
        w2_plane = keep.tile([P, N], U8, name="w2_plane", align_bytes=ALIGN)
        nc.gpsimd.memset(w2_plane[:].bitcast(I32), 0)

        identity = keep.tile([P, P], F32, name="identity", align_bytes=ALIGN)
        make_identity(nc, identity[:])
        def load_w1(name, z, first, last):
            raw = keep.tile([P, last - first, H], F32, name=name, align_bytes=ALIGN)
            rows = w1[z * K_PASS : (z + 1) * K_PASS, :]
            nc.sync.dma_start(out=raw[:], in_=rows.rearrange("(p j) c -> p j c", j=PACK)[:, first:last, :])
            return raw

        def load_x(z):
            window = keep.tile([P, T], U32, name="x_window_%d" % z, align_bytes=ALIGN)
            nc.sync.dma_start(
                out=window[:].bitcast(I32),
                in_=x_words[z].rearrange("p n r -> p (n r)").bitcast(I32),
            )
            return window

        x_window = [load_x(0)]
        nc.sync.dma_start(offsets[:], offs)
        nc.sync.dma_start(out=gate_cols[:], in_=gate[0].rearrange("(p r) -> p r", r=PACK))
        for q in range(QUADRANTS):
            nc.sync.dma_start(
                out=x_scale_window[QUADRANT * q : QUADRANT * q + SCALE_ROWS * PASSES, :].bitcast(I32),
                in_=x_scales[:, SCALE_ROWS * q : SCALE_ROWS * (q + 1), :].bitcast(I32),
            )
        gate_spread = psum.tile([P, PACK, P], F32, name="gate_spread", tag="y_bank_1_1")
        for r in range(PACK):
            nc.tensor.transpose(gate_spread[:, r, :], gate_cols[:, r : r + 1].to_broadcast([P, P]), identity[:])
        gate_all = keep.tile([P, S], F32, name="gate_all", align_bytes=ALIGN)
        nc.scalar.copy(out=gate_all[:].rearrange("p (j r) -> p j r", r=PACK), in_=gate_spread[:].rearrange("p r j -> p j r"))

        w1_first = load_w1("w1_first", 0, 0, PACK)
        w1_left = load_w1("w1_left", 1, 0, 2)
        w1_right = load_w1("w1_right", 1, 2, PACK)
        x_window.append(load_x(1))

        x_plane = keep.tile([P, S], U8, name="x_plane", align_bytes=ALIGN)
        nc.vector.tensor_copy(x_plane[:], x_scale_window[:].indirect(offsets[:]))

        grouped = [
            keep.tile([P, PACK, P, PACK], BF16, name="w1_grouped_%d" % z, align_bytes=ALIGN) for z in range(PASSES)
        ]
        w1_codes = [keep.tile([P, H], U32, name="w1_codes_%d" % z, align_bytes=ALIGN) for z in range(PASSES)]
        w1_plane = [keep.tile([P, H], U8, name="w1_plane_%d" % z, align_bytes=ALIGN) for z in range(PASSES)]

        def round_w1(copy, raw, z, first_j, pair, ms=slice(0, P)):
            ts = slice(2 * pair, 2 * pair + 2)
            dst = grouped[z][:, ts, ms, first_j : first_j + raw.shape[1]].rearrange("p t m j -> p m j t")
            src = raw[:].rearrange("p j (m t) -> p m j t", t=PACK)[:, ms, :, ts]
            copy(out=dst, in_=src)

        def quantize_w1(z, first_t, last_t):
            nc.vector.quantize_mx(
                out=w1_codes[z][:, first_t * P : last_t * P].bitcast(FP8X4),
                scales=w1_plane[z][:, first_t * P : last_t * P],
                in_=grouped[z][:, first_t:last_t, :, :].rearrange("p t m j -> p (t m j)"),
            )

        round_w1(nc.vector.tensor_copy, w1_first, 0, 0, 0)
        round_w1(nc.scalar.copy, w1_first, 0, 0, 1)
        quantize_w1(0, 0, 2)
        round_w1(nc.vector.tensor_copy, w1_left, 1, 0, 0)
        round_w1(nc.scalar.copy, w1_left, 1, 0, 1)
        quantize_w1(0, 2, PACK)
        stream = [keep.tile([P, T], F32, name="stream_%d" % b, align_bytes=ALIGN) for b in range(2)]
        nc.sync.dma_start(out=stream[UPPER][:], in_=res[0:P, :])
        nc.sync.dma_start(out=stream[LOWER][:], in_=res[P:N, :])
        w2_codes = keep.tile([P, N], U32, name="w2_codes", align_bytes=ALIGN)
        nc.sync.dma_start(
            out=w2_codes[:].bitcast(I32),
            in_=w2_words[0].rearrange("p n r -> p (n r)").bitcast(I32),
        )
        for q in range(QUADRANTS):
            nc.sync.dma_start(
                out=w2_plane[QUADRANT * q : QUADRANT * q + SCALE_ROWS, :].bitcast(I32),
                in_=w2_scales[0, SCALE_ROWS * q : SCALE_ROWS * (q + 1), :].bitcast(I32),
            )

        x_codes = [keep.tile([P, S], U32, name="x_codes_0", align_bytes=ALIGN)]
        nc.vector.tensor_copy(x_codes[0][:], x_window[0][:].indirect(offsets[:]))

        h_tags = ["h_a", "h_b", "h_c", "h_d"]
        h_banks = [psum.tile([P, PACK, CHUNK], F32, name="h_bank_%d" % c, tag=h_tags[c]) for c in range(CHUNKS)]

        def first_product(c, t, z):
            cols = slice(c * CHUNK, (c + 1) * CHUNK)
            units = slice(t * P, (t + 1) * P)
            nc.tensor.matmul_mx(
                out=h_banks[c][:, t, :],
                lhsT=w1_codes[z][:, units].bitcast(FP8X4),
                lhsT_scale=w1_plane[z][:, units],
                rhs=(x_first[:] if (z, c) == (1, 0) else x_codes[z][:, cols]).bitcast(FP8X4),
                rhs_scale=x_plane[SCALE_ROWS * z : P, cols],
                start=(z == 0 and t == 0),
                stop=(z == PASSES - 1 and t == PACK - 1),
            )

        for t in range(PACK):
            for c in range(CHUNKS):
                first_product(c, t, 0)

        round_w1(nc.vector.tensor_copy, w1_right, 1, 2, 0)
        round_w1(nc.scalar.copy, w1_right, 1, 2, 1, slice(0, SCALAR_M))
        round_w1(nc.vector.tensor_copy, w1_right, 1, 2, 1, slice(SCALAR_M, P))
        quantize_w1(1, 0, 2)
        quantize_w1(1, 2, PACK)

        x_first = keep.tile([P, CHUNK], U32, name="x_first", align_bytes=ALIGN)
        x_codes.append(keep.tile([P, S], U32, name="x_codes_1", tag="w1_right", align_bytes=ALIGN))
        nc.vector.tensor_copy(x_first[:], x_window[1][:].indirect(entries(0, CHUNK)))
        nc.vector.tensor_copy(x_codes[1][:, CHUNK:HALF_LIST], x_window[1][:].indirect(entries(CHUNK, HALF_LIST)))
        nc.vector.tensor_copy(x_codes[1][:, HALF_LIST:S], x_window[1][:].indirect(entries(HALF_LIST, S)))

        old = [keep.tile([P, S], F32, name="old_%d" % b, align_bytes=ALIGN) for b in range(2)]

        def fetch_on_scalar(b, first, last):
            nc.scalar.activation(old[b][:, first:last], stream[b][:].indirect(entries(first, last)), COPY)

        def fetch_on_vector(b, first, last):
            nc.vector.tensor_copy(old[b][:, first:last], stream[b][:].indirect(entries(first, last)))

        gated = keep.tile([P, 2 * S], F32, name="gated", align_bytes=ALIGN)
        h_values = [keep.tile([P, CHUNK * PACK], BF16, name="h_%d" % c, align_bytes=ALIGN)[:] for c in range(CHUNKS - 1)]
        h_values.append(gated[:, S : S + HALF_LIST].bitcast(BF16))
        h_codes = {}
        h_plane = [keep.tile([P, CHUNK], U8, name="h_plane_%d" % c, align_bytes=ALIGN) for c in range(CHUNKS)]
        y_first = psum.tile([P, CHUNK], F32, name="y_first", tag="y_bank_0_1")
        y_banks = [
            [psum.tile([P, HALF_LIST], F32, name="y_bank_%d_%d" % (b, half)) for half in range(2)] for b in range(2)
        ]
        new_upper = keep.tile([P, S], F32, name="new_upper", align_bytes=ALIGN)

        def gelu_of(c):
            for t in range(PACK):
                first_product(c, t, 1)
            nc.scalar.activation(h_values[c].rearrange("p (n t) -> p n t", t=PACK), h_banks[c][:].rearrange("p t n -> p n t"), GELU)

        def second_product(c, tag):
            h_codes[c] = keep.tile([P, CHUNK], U32, name="h_codes", tag=tag, align_bytes=ALIGN)
            nc.vector.quantize_mx(
                out=h_codes[c][:].bitcast(FP8X4), scales=h_plane[c][:], in_=h_values[c]
            )
            for b in range(2):
                rows = slice(b * P, (b + 1) * P)
                nc.tensor.matmul_mx(
                    out=y_first[:] if (b, c) == (UPPER, 0) else y_banks[b][c // 2][:, (c % 2) * CHUNK : (c % 2 + 1) * CHUNK],
                    lhsT=w2_codes[:, rows].bitcast(FP8X4),
                    lhsT_scale=w2_plane[:, rows],
                    rhs=h_codes[c][:].bitcast(FP8X4),
                    rhs_scale=h_plane[c][:],
                    start=True,
                    stop=True,
                )

        def gate_product(b, half, into):
            cols = slice(half * HALF_LIST, (half + 1) * HALF_LIST)
            nc.vector.tensor_tensor(into, y_banks[b][half][:], gate_all[:, cols], MULT)

        def upper_sum(first, last, update):
            nc.vector.tensor_tensor(new_upper[:, first:last], update, old[UPPER][:, first:last], ADD)

        def put_upper(first, last):
            nc.scalar.activation(stream[UPPER][:].indirect(entries(first, last)), new_upper[:, first:last], COPY)

        def put_lower(first, last):
            nc.vector.tensor_tensor(
                stream[LOWER][:].indirect(entries(first, last)), gated[:, S + first : S + last], old[LOWER][:, first:last], ADD
            )

        fetch_on_vector(UPPER, 0, S)
        for c in range(CHUNKS):
            gelu_of(c)
        fetch_on_scalar(LOWER, SHORT, S)
        second_product(0, "h_codes_0")
        second_product(1, "h_codes_1")
        fetch_on_vector(LOWER, 0, SHORT)
        nc.vector.tensor_tensor(gated[:, 0:CHUNK], y_first[:], gate_all[:, 0:CHUNK], MULT)
        second_product(2, "h_codes_0")
        nc.vector.tensor_tensor(
            gated[:, CHUNK:HALF_LIST], y_banks[UPPER][0][:, CHUNK:HALF_LIST], gate_all[:, CHUNK:HALF_LIST], MULT
        )
        nc.vector.tensor_tensor(
            stream[UPPER][:].indirect(entries(0, HEAD)), gated[:, 0:HEAD], old[UPPER][:, 0:HEAD], ADD
        )
        second_product(CHUNKS - 1, "h_codes_1")
        upper_sum(HEAD, HALF_LIST, gated[:, HEAD:HALF_LIST])
        gate_product(LOWER, 0, gated[:, S : S + HALF_LIST])
        put_upper(HEAD, HALF_LIST)
        gate_product(UPPER, 1, gated[:, HALF_LIST:S])
        gate_product(LOWER, 1, gated[:, S + HALF_LIST : 2 * S])
        upper_sum(HALF_LIST, S, gated[:, HALF_LIST:S])
        put_upper(HALF_LIST, S)
        nc.sync.dma_start(out=out[0:P, :], in_=stream[UPPER][:])
        put_lower(0, S)
        nc.sync.dma_start(out=out[P:N, :], in_=stream[LOWER][:])
